import numpy as np
import ml_dtypes


def mxq(x, axis, fmt="e4m3"):
    dtype, down = {"e4m3": (ml_dtypes.float8_e4m3fn, 7), "e5m2": (ml_dtypes.float8_e5m2, 14)}[fmt]
    v = np.moveaxis(np.asarray(x, np.float32).astype(ml_dtypes.bfloat16).astype(np.float64), axis, -1)
    blocks = v.reshape(v.shape[:-1] + (-1, 32))
    amax = np.abs(blocks).max(-1, keepdims=True)
    byte = np.maximum(np.where(amax > 0, np.frexp(amax)[1] - 1 + 127, 0) - down, 1)
    scale = np.exp2(byte - 127.0)
    codes = (blocks / scale).astype(np.float32).astype(dtype).astype(np.float64)
    return np.moveaxis((codes * scale).reshape(v.shape), -1, axis)


WIDE = False


def mx_kscale(k):
    if not WIDE:
        return np.ones(k)
    levels = np.array([30, -30])
    if k % 512:
        return np.exp2(np.random.permutation(np.resize(levels, k // 32))).repeat(32)
    a = np.empty((k // 512, 16))
    for p in range(k // 512):
        a[p, :8] = np.random.permutation(np.resize(levels, 8))
        for g in range(8):
            far = levels[np.abs(levels - a[p, g]) >= 10]
            a[p, g + 8] = far[np.random.randint(len(far))]
    return np.exp2(a.ravel()).repeat(32)


def f64(x):
    return np.asarray(x).astype(np.float64)


def striped(idx):
    return np.tile(idx.reshape(-1, 16).T, (8, 1)).astype(np.uint16)


def unstriped(offs):
    return offs[:16].T.reshape(-1).astype(np.int64)


E2M1 = np.array([0.0, 0.5, 1.0, 1.5, 2.0, 3.0, 4.0, 6.0, -0.0, -0.5, -1.0, -1.5, -2.0, -3.0, -4.0, -6.0])


def pack_weight(w, fmt):
    k, n = w.shape
    w = f64(np.asarray(w, np.float32).astype(ml_dtypes.bfloat16)).reshape(k // 32, 32, n)
    amax = np.abs(w).max(1)
    if fmt == "e4m3":
        byte = np.frexp(amax)[1] - 1 + 127 - 7
    else:
        mant, ex = np.frexp(amax / 6.0)
        byte = np.where(mant > 0.5, ex, ex - 1) + 127
    byte = np.clip(np.where(amax > 0, byte, 1), 1, 254)
    scaled = (w * np.exp2(127.0 - byte)[:, None, :]).reshape(k, n).astype(np.float32)
    by_word = np.ascontiguousarray(scaled.reshape(k // 512, 128, 4, n).transpose(0, 1, 3, 2))
    if fmt == "e4m3":
        words = by_word.astype(ml_dtypes.float8_e4m3fn).view(np.uint8)
    else:
        c = by_word.astype(ml_dtypes.float4_e2m1fn).view(np.uint8) & 0xF
        words = (c[..., 0::2] | (c[..., 1::2] << 4)).reshape(k // 512, 128, 2 * n)
    return np.ascontiguousarray(words), np.ascontiguousarray(byte.astype(np.uint8).reshape(k // 512, 16, n))


def unpack_weight(words, scales, fmt):
    g, _, n = scales.shape
    words = np.ascontiguousarray(words).reshape(g, 128, n, -1)
    if fmt == "e4m3":
        vals = words.view(ml_dtypes.float8_e4m3fn).astype(np.float64)
    else:
        nib = np.empty((g, 128, n, 4), np.uint8)
        nib[..., 0::2] = words & 0xF
        nib[..., 1::2] = words >> 4
        vals = E2M1[nib]
    vals = vals * np.repeat(np.exp2(scales.astype(np.float64) - 127.0), 8, axis=1)[..., None]
    return vals.transpose(0, 1, 3, 2).reshape(g * 512, n)


K, T, E, C, N = 128, 2048, 8, 512, 512


def by_expert(wq, xq):
    return np.concatenate([wq[e].T @ xq[:, e * C:(e + 1) * C] for e in range(E)], axis=1)


def setup_inputs():
    n = np.random.standard_normal
    s = mx_kscale(N)[:, None]
    first = np.random.permutation(np.repeat(np.arange(E), T // E))
    second = (first + 1 + np.random.permutation(np.repeat(np.arange(E - 1), -(-T // (E - 1)))[:T])) % E
    while np.bincount(second, minlength=E).max() != T // E:
        load = np.bincount(second, minlength=E); hi, lo = int(load.argmax()), int(load.argmin())
        t = np.flatnonzero((second == hi) & (first != lo))[0]; second[t] = lo
    slot_token = np.empty(E * C, np.int64); pos = np.empty((2, T), np.int64); fill = np.zeros(E, np.int64)
    place = np.stack([np.random.permutation(C) for _ in range(E)])
    for r, deal in enumerate((first, second)):
        for t in np.random.permutation(T):
            e = deal[t]; j = e * C + place[e, fill[e]]; fill[e] += 1; slot_token[j] = t; pos[r, t] = j
    g = np.random.uniform(0.2, 0.8, T)
    w_slot = np.empty(E * C); w_slot[pos[0]] = g; w_slot[pos[1]] = 1.0 - g
    w = [pack_weight(m, "e2m1") for m in n((E, N, K)) / np.sqrt(N) / s[None]]
    return {
        "dyT": (n((N, T)) * s).astype(np.float32),
        "w_words": np.stack([m[0] for m in w]),
        "w_scales": np.stack([m[1] for m in w]),
        "gate": np.tile(w_slot, (N, 1)).astype(np.float32),
        "offs": striped(slot_token),
        "pos1": striped(pos[0]),
        "pos2": striped(pos[1]),
    }


def reference(dyT, w_words, w_scales, gate, offs, pos1, pos2):
    idx = unstriped(offs)
    w = np.stack([unpack_weight(w_words[e], w_scales[e], "e2m1") for e in range(E)])
    gq = mxq(f64(gate) * f64(dyT)[:, idx], 0, "e5m2")
    dx = by_expert(w, gq)
    return dx[:, unstriped(pos1)] + dx[:, unstriped(pos2)]

@@ -1,0 +1,160 @@
+from contextlib import ExitStack
+
+import concourse.mybir as mybir
+
+FLOPS = 2 * 512 * 128 * 4096
+BYTES = 4 * 512 * 2048 + 8 * 128 * 256 + 8 * 16 * 128 + 4 * 4096 + 128 * 512 * 2 + 4 * 128 * 2048
+
+P = 128
+T, E, C, N, K = 2048, 8, 512, 512, 128
+SLOTS = E * C
+R = 4
+
+F32 = mybir.dt.float32
+BF16 = mybir.dt.bfloat16
+I32 = mybir.dt.int32
+U32 = mybir.dt.uint32
+U16 = mybir.dt.uint16
+U8 = mybir.dt.uint8
+E5M2X4 = mybir.dt.float8_e5m2_x4
+E2M1X4 = mybir.dt.float4_e2m1fn_x4
+MULT = mybir.AluOpType.mult
+ADD = mybir.AluOpType.add
+
+SIZES = (1664, 1280, 768, 384)
+HEAD = ((0, 256), (256, 768), (768, 1664))
+
+
+def tile_moe_bdx_lin_none_kernel(tc, dyT, w_words, w_scales, gate, offs, pos1, pos2, out):
+    nc = tc.nc
+    with ExitStack() as ctx:
+        keep = ctx.enter_context(tc.tile_pool(name="keep", bufs=1))
+        stage = ctx.enter_context(tc.tile_pool(name="stage", bufs=2))
+        psum = ctx.enter_context(tc.psum_pool(name="psum", bufs=4))
+
+        offs_sb = keep.tile([P, SLOTS // 16], U16, name="offs_sb")
+        pos1_sb = keep.tile([P, T // 16], U16, name="pos1_sb")
+        pos2_sb = keep.tile([P, T // 16], U16, name="pos2_sb")
+        planes = [keep.tile([P, T], F32, name=f"plane{t}") for t in range(R)]
+        gate_sb = keep.tile([P, SLOTS], F32, name="gate_sb")
+        w_sb = keep.tile([P, E * 2 * K], U8, name="w_sb", align_bytes=64)
+        ws_sb = keep.tile([P, E * K], U8, name="ws_sb", align_bytes=64)
+        dx = keep.tile([P, SLOTS], F32, name="dx")
+        codes = keep.tile([P, SLOTS], U32, name="codes", align_bytes=64)
+        scales = keep.tile([P, SLOTS], U8, name="scales", align_bytes=64)
+        res1 = keep.tile([P, T], F32, name="res1")
+        res2 = keep.tile([P, T], F32, name="res2")
+        total = keep.tile([P, T], F32, name="total")
+
+        nc.gpsimd.memset(ws_sb[:].bitcast(I32), 0)
+
+        rows = dyT.rearrange("(p t) w -> p t w", t=R)
+
+        def load_gate(a, b):
+            nc.sync.dma_start(gate_sb[:, a:b], gate[0:P, a:b])
+
+        nc.sync.dma_start(offs_sb[:], offs)
+        nc.sync.dma_start(planes[0][:], rows[:, 0, :])
+        for a, b in HEAD:
+            load_gate(a, b)
+        for t in range(1, R):
+            nc.sync.dma_start(planes[t][:], rows[:, t, :])
+        load_gate(1664, 2944)
+        load_gate(2944, 4096)
+        nc.sync.dma_start(
+            w_sb[:].bitcast(I32).rearrange("p (e n) -> p e n", e=E),
+            w_words.bitcast(I32).rearrange("e a p n -> p (e a) n"),
+        )
+        for q in range(4):
+            nc.sync.dma_start(
+                ws_sb[32 * q : 32 * q + 4, :].bitcast(I32).rearrange("f (e n) -> f e n", e=E),
+                w_scales.bitcast(I32)[:, 0, 4 * q : 4 * q + 4, :].rearrange("e f n -> f e n"),
+            )
+        nc.sync.dma_start(pos1_sb[:], pos1)
+        nc.sync.dma_start(pos2_sb[:], pos2)
+
+        state = {"quantised": 0, "experts": 0}
+
+        def quantise(unit):
+            grouped, base, a, b = unit
+            nc.vector.quantize_mx(
+                out=codes[:, a:b].bitcast(E5M2X4),
+                scales=scales[:, a:b],
+                in_=grouped[:, a - base : b - base, :].rearrange("p c t -> p (c t)"),
+            )
+            state["quantised"] += b - a
+            while (state["experts"] + 1) * C <= state["quantised"]:
+                e = state["experts"]
+                state["experts"] += 1
+                acc = psum.tile([P, C], F32, name="acc")
+                nc.tensor.matmul_mx(
+                    out=acc[:],
+                    lhsT=w_sb[:, e * 2 * K : (e + 1) * 2 * K].bitcast(E2M1X4),
+                    lhsT_scale=ws_sb[:, e * K : (e + 1) * K],
+                    rhs=codes[:, e * C : (e + 1) * C].bitcast(E5M2X4),
+                    rhs_scale=scales[:, e * C : (e + 1) * C],
+                    start=True,
+                    stop=True,
+                )
+                (nc.vector.tensor_copy if e == E - 1 else nc.scalar.copy)(dx[:, e * C : (e + 1) * C], acc[:])
+
+        def interleave(engine_copy, raw, base, a, b):
+            grouped = keep.tile([P, b - a, R], BF16, name=f"grouped{a}", align_bytes=64)
+            engine_copy(
+                grouped[:].rearrange("p (c i) t -> p c t i", i=4),
+                raw[:, :, a - base : b - base].rearrange("p t (c i) -> p c t i", i=4),
+            )
+            units = []
+            first = a
+            while first < b:
+                size = next_size(b - first)
+                units.append((grouped, a, first, first + size))
+                first += size
+            return units
+
+        def next_size(left):
+            for size in (1024, 512, 256, 128, 64, 32):
+                if size <= left:
+                    return size
+
+        pending = []
+        first = 0
+        for size in SIZES:
+            last = first + size
+            raw = stage.tile([P, R, size], F32, name="raw")
+            for t in range(R):
+                for a, b in HEAD if (first == 0 and t == 0) else ((first, last),):
+                    nc.vector.tensor_tensor(
+                        raw[:, t, a - first : b - first],
+                        planes[t][:].indirect(offs_sb[:, a // 16 : b // 16]),
+                        gate_sb[:, a:b],
+                        MULT,
+                    )
+            if last < SLOTS:
+                units = interleave(nc.scalar.copy, raw, first, first, last)
+                while pending:
+                    quantise(pending.pop(0))
+                pending = units
+            else:
+                mid = first + 256
+                by_scalar = interleave(nc.scalar.copy, raw, first, first, mid)
+                by_vector = interleave(nc.vector.tensor_copy, raw, first, mid, last)
+                while pending:
+                    quantise(pending.pop(0))
+                for unit in by_vector + by_scalar:
+                    quantise(unit)
+            first = last
+
+        nc.vector.tensor_copy(res1[:, 0:1024], dx[:].indirect(pos1_sb[:, 0:64]))
+        nc.vector.tensor_copy(res2[:, 0:1024], dx[:].indirect(pos2_sb[:, 0:64]))
+        nc.gpsimd.tensor_tensor(total[:, 0:1024], res1[:, 0:1024], res2[:, 0:1024], ADD)
+        nc.sync.dma_start(out[:, 0:1024], total[:, 0:1024])
+        nc.vector.tensor_copy(res1[:, 1024:2048], dx[:].indirect(pos1_sb[:, 64:128]))
+        nc.vector.tensor_copy(res2[:, 1024:1536], dx[:].indirect(pos2_sb[:, 64:96]))
+        nc.gpsimd.tensor_tensor(total[:, 1024:1536], res1[:, 1024:1536], res2[:, 1024:1536], ADD)
+        nc.sync.dma_start(out[:, 1024:1536], total[:, 1024:1536])
+        nc.vector.tensor_copy(res2[:, 1536:2048], dx[:].indirect(pos2_sb[:, 96:128]))
+        nc.vector.tensor_tensor(total[:, 1536:1792], res1[:, 1536:1792], res2[:, 1536:1792], ADD)
+        nc.sync.dma_start(out[:, 1536:1792], total[:, 1536:1792])
+        nc.vector.tensor_tensor(total[:, 1792:2048], res1[:, 1792:2048], res2[:, 1792:2048], ADD)
+        nc.sync.dma_start(out[:, 1792:2048], total[:, 1792:2048])

@@ -43,7 +43,6 @@ def tile_moe_bdx_lin_none_kernel(tc, dyT, w_words, w_scales, gate, offs, pos1, p
         codes = keep.tile([P, SLOTS], U32, name="codes", align_bytes=64)
         scales = keep.tile([P, SLOTS], U8, name="scales", align_bytes=64)
         res1 = keep.tile([P, T], F32, name="res1")
-        res2 = keep.tile([P, T], F32, name="res2")
         total = keep.tile([P, T], F32, name="total")
 
         nc.gpsimd.memset(ws_sb[:].bitcast(I32), 0)
@@ -145,16 +144,8 @@ def tile_moe_bdx_lin_none_kernel(tc, dyT, w_words, w_scales, gate, offs, pos1, p
                     quantise(unit)
             first = last
 
-        nc.vector.tensor_copy(res1[:, 0:1024], dx[:].indirect(pos1_sb[:, 0:64]))
-        nc.vector.tensor_copy(res2[:, 0:1024], dx[:].indirect(pos2_sb[:, 0:64]))
-        nc.gpsimd.tensor_tensor(total[:, 0:1024], res1[:, 0:1024], res2[:, 0:1024], ADD)
-        nc.sync.dma_start(out[:, 0:1024], total[:, 0:1024])
-        nc.vector.tensor_copy(res1[:, 1024:2048], dx[:].indirect(pos1_sb[:, 64:128]))
-        nc.vector.tensor_copy(res2[:, 1024:1536], dx[:].indirect(pos2_sb[:, 64:96]))
-        nc.gpsimd.tensor_tensor(total[:, 1024:1536], res1[:, 1024:1536], res2[:, 1024:1536], ADD)
-        nc.sync.dma_start(out[:, 1024:1536], total[:, 1024:1536])
-        nc.vector.tensor_copy(res2[:, 1536:2048], dx[:].indirect(pos2_sb[:, 96:128]))
-        nc.vector.tensor_tensor(total[:, 1536:1792], res1[:, 1536:1792], res2[:, 1536:1792], ADD)
-        nc.sync.dma_start(out[:, 1536:1792], total[:, 1536:1792])
-        nc.vector.tensor_tensor(total[:, 1792:2048], res1[:, 1792:2048], res2[:, 1792:2048], ADD)
-        nc.sync.dma_start(out[:, 1792:2048], total[:, 1792:2048])
+        for a, b in ((0, 1280), (1280, 2048)):
+            nc.vector.tensor_copy(res1[:, a:b], dx[:].indirect(pos1_sb[:, a // 16 : b // 16]))
+        for a, b in ((0, 1280), (1280, 1792), (1792, 2048)):
+            nc.vector.tensor_tensor(total[:, a:b], dx[:].indirect(pos2_sb[:, a // 16 : b // 16]), res1[:, a:b], ADD)
+            nc.sync.dma_start(out[:, a:b], total[:, a:b])

@@ -21,16 +21,17 @@ E2M1X4 = mybir.dt.float4_e2m1fn_x4
 MULT = mybir.AluOpType.mult
 ADD = mybir.AluOpType.add
 
-SIZES = (1664, 1280, 768, 384)
-HEAD = ((0, 256), (256, 768), (768, 1664))
+CHUNKS = ((0, 2016), (2016, 3296), (3296, 4096))
+HEAD = ((0, 256), (256, 832), (832, 2016))
+LAST = ((3584, 4096), (3296, 3584))
+QUANT = ((0, 1024), (1024, 2048), (2048, 3072), (3584, 4096), (3072, 3584))
 
 
 def tile_moe_bdx_lin_none_kernel(tc, dyT, w_words, w_scales, gate, offs, pos1, pos2, out):
     nc = tc.nc
     with ExitStack() as ctx:
         keep = ctx.enter_context(tc.tile_pool(name="keep", bufs=1))
-        stage = ctx.enter_context(tc.tile_pool(name="stage", bufs=2))
-        psum = ctx.enter_context(tc.psum_pool(name="psum", bufs=4))
+        psum = ctx.enter_context(tc.psum_pool(name="psum", bufs=8))
 
         offs_sb = keep.tile([P, SLOTS // 16], U16, name="offs_sb")
         pos1_sb = keep.tile([P, T // 16], U16, name="pos1_sb")
@@ -53,13 +54,12 @@ def tile_moe_bdx_lin_none_kernel(tc, dyT, w_words, w_scales, gate, offs, pos1, p
             nc.sync.dma_start(gate_sb[:, a:b], gate[0:P, a:b])
 
         nc.sync.dma_start(offs_sb[:], offs)
-        nc.sync.dma_start(planes[0][:], rows[:, 0, :])
+        nc.sync.dma_start(planes[R - 1][:], rows[:, R - 1, :])
         for a, b in HEAD:
             load_gate(a, b)
-        for t in range(1, R):
+        for t in reversed(range(R - 1)):
             nc.sync.dma_start(planes[t][:], rows[:, t, :])
-        load_gate(1664, 2944)
-        load_gate(2944, 4096)
+        load_gate(CHUNKS[1][0], SLOTS)
         nc.sync.dma_start(
             w_sb[:].bitcast(I32).rearrange("p (e n) -> p e n", e=E),
             w_words.bitcast(I32).rearrange("e a p n -> p (e a) n"),
@@ -72,19 +72,40 @@ def tile_moe_bdx_lin_none_kernel(tc, dyT, w_words, w_scales, gate, offs, pos1, p
         nc.sync.dma_start(pos1_sb[:], pos1)
         nc.sync.dma_start(pos2_sb[:], pos2)
 
-        state = {"quantised": 0, "experts": 0}
+        grouped = keep.tile([P, SLOTS, R], BF16, name="grouped", align_bytes=64)
 
-        def quantise(unit):
-            grouped, base, a, b = unit
+        def interleave(raw, base, a, b):
+            nc.scalar.copy(
+                grouped[:, a:b, :].rearrange("p (c i) t -> p c t i", i=4),
+                raw[:, :, a - base : b - base].rearrange("p t (c i) -> p c t i", i=4),
+            )
+
+        for first, last in CHUNKS:
+            raw = keep.tile([P, R, last - first], F32, name=f"raw{first}")
+            for t in reversed(range(R)):
+                pieces = ((first, last),)
+                if first == 0 and t == R - 1:
+                    pieces = HEAD
+                if last == SLOTS and t == 0:
+                    pieces = LAST
+                for a, b in pieces:
+                    nc.vector.tensor_tensor(
+                        raw[:, t, a - first : b - first],
+                        planes[t][:].indirect(offs_sb[:, a // 16 : b // 16]),
+                        gate_sb[:, a:b],
+                        MULT,
+                    )
+                    if t == 0:
+                        interleave(raw, first, a, b)
+
+        late = []
+        for a, b in QUANT:
             nc.vector.quantize_mx(
                 out=codes[:, a:b].bitcast(E5M2X4),
                 scales=scales[:, a:b],
-                in_=grouped[:, a - base : b - base, :].rearrange("p c t -> p (c t)"),
+                in_=grouped[:, a:b, :].rearrange("p c t -> p (c t)"),
             )
-            state["quantised"] += b - a
-            while (state["experts"] + 1) * C <= state["quantised"]:
-                e = state["experts"]
-                state["experts"] += 1
+            for e in range(a // C, b // C):
                 acc = psum.tile([P, C], F32, name="acc")
                 nc.tensor.matmul_mx(
                     out=acc[:],
@@ -95,54 +116,12 @@ def tile_moe_bdx_lin_none_kernel(tc, dyT, w_words, w_scales, gate, offs, pos1, p
                     start=True,
                     stop=True,
                 )
-                (nc.vector.tensor_copy if e == E - 1 else nc.scalar.copy)(dx[:, e * C : (e + 1) * C], acc[:])
-
-        def interleave(engine_copy, raw, base, a, b):
-            grouped = keep.tile([P, b - a, R], BF16, name=f"grouped{a}", align_bytes=64)
-            engine_copy(
-                grouped[:].rearrange("p (c i) t -> p c t i", i=4),
-                raw[:, :, a - base : b - base].rearrange("p t (c i) -> p c t i", i=4),
-            )
-            units = []
-            first = a
-            while first < b:
-                size = next_size(b - first)
-                units.append((grouped, a, first, first + size))
-                first += size
-            return units
-
-        def next_size(left):
-            for size in (1024, 512, 256, 128, 64, 32):
-                if size <= left:
-                    return size
-
-        pending = []
-        first = 0
-        for size in SIZES:
-            last = first + size
-            raw = stage.tile([P, R, size], F32, name="raw")
-            for t in range(R):
-                for a, b in HEAD if (first == 0 and t == 0) else ((first, last),):
-                    nc.vector.tensor_tensor(
-                        raw[:, t, a - first : b - first],
-                        planes[t][:].indirect(offs_sb[:, a // 16 : b // 16]),
-                        gate_sb[:, a:b],
-                        MULT,
-                    )
-            if last < SLOTS:
-                units = interleave(nc.scalar.copy, raw, first, first, last)
-                while pending:
-                    quantise(pending.pop(0))
-                pending = units
-            else:
-                mid = first + 256
-                by_scalar = interleave(nc.scalar.copy, raw, first, first, mid)
-                by_vector = interleave(nc.vector.tensor_copy, raw, first, mid, last)
-                while pending:
-                    quantise(pending.pop(0))
-                for unit in by_vector + by_scalar:
-                    quantise(unit)
-            first = last
+                if e < E - 2:
+                    nc.scalar.copy(dx[:, e * C : (e + 1) * C], acc[:])
+                else:
+                    late.append((e, acc))
+        for e, acc in late:
+            nc.vector.tensor_copy(dx[:, e * C : (e + 1) * C], acc[:])
 
         for a, b in ((0, 1280), (1280, 2048)):
             nc.vector.tensor_copy(res1[:, a:b], dx[:].indirect(pos1_sb[:, a // 16 : b // 16]))

@@ -23,8 +23,8 @@ ADD = mybir.AluOpType.add
 
 CHUNKS = ((0, 2016), (2016, 3296), (3296, 4096))
 HEAD = ((0, 256), (256, 832), (832, 2016))
-LAST = ((3584, 4096), (3296, 3584))
-QUANT = ((0, 1024), (1024, 2048), (2048, 3072), (3584, 4096), (3072, 3584))
+LAST = ((3296, 3584), (3584, 4096))
+QUANT = ((0, 1024), (1024, 2048), (2048, 3072), (3072, 3584), (3584, 3840), (3840, 4096))
 
 
 def tile_moe_bdx_lin_none_kernel(tc, dyT, w_words, w_scales, gate, offs, pos1, pos2, out):
@@ -40,7 +40,7 @@ def tile_moe_bdx_lin_none_kernel(tc, dyT, w_words, w_scales, gate, offs, pos1, p
         gate_sb = keep.tile([P, SLOTS], F32, name="gate_sb")
         w_sb = keep.tile([P, E * 2 * K], U8, name="w_sb", align_bytes=64)
         ws_sb = keep.tile([P, E * K], U8, name="ws_sb", align_bytes=64)
-        dx = keep.tile([P, SLOTS], F32, name="dx")
+        dx = keep.tile([P, SLOTS], F32, name="dx", align_bytes=64)
         codes = keep.tile([P, SLOTS], U32, name="codes", align_bytes=64)
         scales = keep.tile([P, SLOTS], U8, name="scales", align_bytes=64)
         res1 = keep.tile([P, T], F32, name="res1")
@@ -54,10 +54,10 @@ def tile_moe_bdx_lin_none_kernel(tc, dyT, w_words, w_scales, gate, offs, pos1, p
             nc.sync.dma_start(gate_sb[:, a:b], gate[0:P, a:b])
 
         nc.sync.dma_start(offs_sb[:], offs)
-        nc.sync.dma_start(planes[R - 1][:], rows[:, R - 1, :])
+        nc.sync.dma_start(planes[0][:], rows[:, 0, :])
         for a, b in HEAD:
             load_gate(a, b)
-        for t in reversed(range(R - 1)):
+        for t in range(1, R):
             nc.sync.dma_start(planes[t][:], rows[:, t, :])
         load_gate(CHUNKS[1][0], SLOTS)
         nc.sync.dma_start(
@@ -72,21 +72,26 @@ def tile_moe_bdx_lin_none_kernel(tc, dyT, w_words, w_scales, gate, offs, pos1, p
         nc.sync.dma_start(pos1_sb[:], pos1)
         nc.sync.dma_start(pos2_sb[:], pos2)
 
-        grouped = keep.tile([P, SLOTS, R], BF16, name="grouped", align_bytes=64)
+        grouped = keep.tile([P, SLOTS - C, R], BF16, name="grouped", align_bytes=64)
+        grouped_last = dx[:, (E - 3) * C : (E - 1) * C].bitcast(BF16).rearrange("p (c t) -> p c t", t=R)
+
+        def rounded(a, b):
+            base = SLOTS - C
+            return grouped[:, a:b, :] if b <= base else grouped_last[:, a - base : b - base, :]
 
         def interleave(raw, base, a, b):
             nc.scalar.copy(
-                grouped[:, a:b, :].rearrange("p (c i) t -> p c t i", i=4),
+                rounded(a, b).rearrange("p (c i) t -> p c t i", i=4),
                 raw[:, :, a - base : b - base].rearrange("p t (c i) -> p c t i", i=4),
             )
 
         for first, last in CHUNKS:
             raw = keep.tile([P, R, last - first], F32, name=f"raw{first}")
-            for t in reversed(range(R)):
+            for t in range(R):
                 pieces = ((first, last),)
-                if first == 0 and t == R - 1:
+                if first == 0 and t == 0:
                     pieces = HEAD
-                if last == SLOTS and t == 0:
+                if last == SLOTS and t == R - 1:
                     pieces = LAST
                 for a, b in pieces:
                     nc.vector.tensor_tensor(
@@ -95,7 +100,7 @@ def tile_moe_bdx_lin_none_kernel(tc, dyT, w_words, w_scales, gate, offs, pos1, p
                         gate_sb[:, a:b],
                         MULT,
                     )
-                    if t == 0:
+                    if t == R - 1:
                         interleave(raw, first, a, b)
 
         late = []
@@ -103,25 +108,27 @@ def tile_moe_bdx_lin_none_kernel(tc, dyT, w_words, w_scales, gate, offs, pos1, p
             nc.vector.quantize_mx(
                 out=codes[:, a:b].bitcast(E5M2X4),
                 scales=scales[:, a:b],
-                in_=grouped[:, a:b, :].rearrange("p c t -> p (c t)"),
+                in_=rounded(a, b).rearrange("p c t -> p (c t)"),
             )
-            for e in range(a // C, b // C):
+            for lo in range(a, b, C):
+                hi = min(lo + C, b)
+                e = lo // C
                 acc = psum.tile([P, C], F32, name="acc")
                 nc.tensor.matmul_mx(
                     out=acc[:],
                     lhsT=w_sb[:, e * 2 * K : (e + 1) * 2 * K].bitcast(E2M1X4),
                     lhsT_scale=ws_sb[:, e * K : (e + 1) * K],
-                    rhs=codes[:, e * C : (e + 1) * C].bitcast(E5M2X4),
-                    rhs_scale=scales[:, e * C : (e + 1) * C],
+                    rhs=codes[:, hi - C : hi].bitcast(E5M2X4),
+                    rhs_scale=scales[:, hi - C : hi],
                     start=True,
                     stop=True,
                 )
-                if e < E - 2:
-                    nc.scalar.copy(dx[:, e * C : (e + 1) * C], acc[:])
+                if e < E - 3:
+                    nc.scalar.copy(dx[:, lo:hi], acc[:])
                 else:
-                    late.append((e, acc))
-        for e, acc in late:
-            nc.vector.tensor_copy(dx[:, e * C : (e + 1) * C], acc[:])
+                    late.append((dx[:, lo:hi], acc[:, C - (hi - lo) : C]))
+        for engine_copy, (slots, sums) in zip((nc.scalar.copy, nc.vector.tensor_copy) * 2, late):
+            engine_copy(slots, sums)
 
         for a, b in ((0, 1280), (1280, 2048)):
             nc.vector.tensor_copy(res1[:, a:b], dx[:].indirect(pos1_sb[:, a // 16 : b // 16]))

@@ -24,7 +24,7 @@ ADD = mybir.AluOpType.add
 CHUNKS = ((0, 2016), (2016, 3296), (3296, 4096))
 HEAD = ((0, 256), (256, 832), (832, 2016))
 LAST = ((3296, 3584), (3584, 4096))
-QUANT = ((0, 1024), (1024, 2048), (2048, 3072), (3072, 3584), (3584, 3840), (3840, 4096))
+QUANT = tuple((e * C, (e + 1) * C) for e in range(E - 1)) + ((3584, 3840), (3840, 4096))
 
 
 def tile_moe_bdx_lin_none_kernel(tc, dyT, w_words, w_scales, gate, offs, pos1, pos2, out):

@@ -127,11 +127,11 @@ def tile_moe_bdx_lin_none_kernel(tc, dyT, w_words, w_scales, gate, offs, pos1, p
                     nc.scalar.copy(dx[:, lo:hi], acc[:])
                 else:
                     late.append((dx[:, lo:hi], acc[:, C - (hi - lo) : C]))
-        for engine_copy, (slots, sums) in zip((nc.scalar.copy, nc.vector.tensor_copy) * 2, late):
+        for engine_copy, (slots, sums) in zip((nc.scalar.copy, nc.vector.tensor_copy, nc.vector.tensor_copy, nc.scalar.copy), late):
             engine_copy(slots, sums)
 
-        for a, b in ((0, 1280), (1280, 2048)):
+        for a, b in ((0, 1088), (1088, 2048)):
             nc.vector.tensor_copy(res1[:, a:b], dx[:].indirect(pos1_sb[:, a // 16 : b // 16]))
-        for a, b in ((0, 1280), (1280, 1792), (1792, 2048)):
+        for a, b in ((0, 1088), (1088, 1664), (1664, 1920), (1920, 2048)):
             nc.vector.tensor_tensor(total[:, a:b], dx[:].indirect(pos2_sb[:, a // 16 : b // 16]), res1[:, a:b], ADD)
             nc.sync.dma_start(out[:, a:b], total[:, a:b])

@@ -53,8 +53,8 @@ def tile_moe_bdx_lin_none_kernel(tc, dyT, w_words, w_scales, gate, offs, pos1, p
         def load_gate(a, b):
             nc.sync.dma_start(gate_sb[:, a:b], gate[0:P, a:b])
 
-        nc.sync.dma_start(offs_sb[:], offs)
         nc.sync.dma_start(planes[0][:], rows[:, 0, :])
+        nc.sync.dma_start(offs_sb[:], offs)
         for a, b in HEAD:
             load_gate(a, b)
         for t in range(1, R):

@@ -21,9 +21,11 @@ E2M1X4 = mybir.dt.float4_e2m1fn_x4
 MULT = mybir.AluOpType.mult
 ADD = mybir.AluOpType.add
 
-CHUNKS = ((0, 2016), (2016, 3296), (3296, 4096))
-HEAD = ((0, 256), (256, 832), (832, 2016))
-LAST = ((3296, 3584), (3584, 4096))
+GATHERS = (
+    (0, 0, 256), (0, 256, 832), (0, 832, 2176),
+    (1, 0, 1152), (2, 0, 2848), (3, 0, 3296),
+    (1, 1152, 3584), (0, 2176, 4096), (2, 2848, 4096), (3, 3296, 4096), (1, 3584, 4096),
+)
 QUANT = tuple((e * C, (e + 1) * C) for e in range(E - 1)) + ((3584, 3840), (3840, 4096))
 
 
@@ -36,7 +38,8 @@ def tile_moe_bdx_lin_none_kernel(tc, dyT, w_words, w_scales, gate, offs, pos1, p
         offs_sb = keep.tile([P, SLOTS // 16], U16, name="offs_sb")
         pos1_sb = keep.tile([P, T // 16], U16, name="pos1_sb")
         pos2_sb = keep.tile([P, T // 16], U16, name="pos2_sb")
-        planes = [keep.tile([P, T], F32, name=f"plane{t}") for t in range(R)]
+        widths = [max(T, 32 + max(b - a for u, a, b in GATHERS if u == t)) for t in range(R)]
+        planes = [keep.tile([P, widths[t]], F32, name=f"plane{t}") for t in range(R)]
         gate_sb = keep.tile([P, SLOTS], F32, name="gate_sb")
         w_sb = keep.tile([P, E * 2 * K], U8, name="w_sb", align_bytes=64)
         ws_sb = keep.tile([P, E * K], U8, name="ws_sb", align_bytes=64)
@@ -47,19 +50,26 @@ def tile_moe_bdx_lin_none_kernel(tc, dyT, w_words, w_scales, gate, offs, pos1, p
         total = keep.tile([P, T], F32, name="total")
 
         nc.gpsimd.memset(ws_sb[:].bitcast(I32), 0)
+        for t in range(R):
+            if widths[t] > T:
+                nc.gpsimd.memset(planes[t][:, T:], 0.0)
 
         rows = dyT.rearrange("(p t) w -> p t w", t=R)
 
         def load_gate(a, b):
             nc.sync.dma_start(gate_sb[:, a:b], gate[0:P, a:b])
 
-        nc.sync.dma_start(planes[0][:], rows[:, 0, :])
+        nc.sync.dma_start(planes[0][:, :T], rows[:, 0, :])
         nc.sync.dma_start(offs_sb[:], offs)
-        for a, b in HEAD:
-            load_gate(a, b)
-        for t in range(1, R):
-            nc.sync.dma_start(planes[t][:], rows[:, t, :])
-        load_gate(CHUNKS[1][0], SLOTS)
+        loaded, have = {0}, 0
+        for t, a, b in GATHERS[:6]:
+            if b > have:
+                load_gate(have, b)
+                have = b
+            if t not in loaded:
+                nc.sync.dma_start(planes[t][:, :T], rows[:, t, :])
+                loaded.add(t)
+        load_gate(have, SLOTS)
         nc.sync.dma_start(
             w_sb[:].bitcast(I32).rearrange("p (e n) -> p e n", e=E),
             w_words.bitcast(I32).rearrange("e a p n -> p (e a) n"),
@@ -82,26 +92,22 @@ def tile_moe_bdx_lin_none_kernel(tc, dyT, w_words, w_scales, gate, offs, pos1, p
         def interleave(raw, base, a, b):
             nc.scalar.copy(
                 rounded(a, b).rearrange("p (c i) t -> p c t i", i=4),
-                raw[:, :, a - base : b - base].rearrange("p t (c i) -> p c t i", i=4),
+                raw[:, :, a // 4 : b // 4, :].rearrange("p t c i -> p c t i"),
             )
 
-        for first, last in CHUNKS:
-            raw = keep.tile([P, R, last - first], F32, name=f"raw{first}")
-            for t in range(R):
-                pieces = ((first, last),)
-                if first == 0 and t == 0:
-                    pieces = HEAD
-                if last == SLOTS and t == R - 1:
-                    pieces = LAST
-                for a, b in pieces:
-                    nc.vector.tensor_tensor(
-                        raw[:, t, a - first : b - first],
-                        planes[t][:].indirect(offs_sb[:, a // 16 : b // 16]),
-                        gate_sb[:, a:b],
-                        MULT,
-                    )
-                    if t == R - 1:
-                        interleave(raw, first, a, b)
+        raw = keep.tile([P, R, SLOTS // 4, 4], F32, name="raw")
+        done = [0] * R
+        for t, a, b in GATHERS:
+            nc.vector.tensor_tensor(
+                raw[:, t, a // 4 : b // 4, :],
+                planes[t][:].indirect(offs_sb[:, a // 16 : b // 16]),
+                gate_sb[:, a:b].rearrange("p (c i) -> p c i", i=4),
+                MULT,
+            )
+            front = min(done)
+            done[t] = b
+            if min(done) > front:
+                interleave(raw, 0, front, min(done))
 
         late = []
         for a, b in QUANT:

@@ -1,6 +1,7 @@
 from contextlib import ExitStack
 
 import concourse.mybir as mybir
+from concourse.masks import make_identity
 
 FLOPS = 2 * 512 * 128 * 4096
 BYTES = 4 * 512 * 2048 + 8 * 128 * 256 + 8 * 16 * 128 + 4 * 4096 + 128 * 512 * 2 + 4 * 128 * 2048
@@ -21,8 +22,11 @@ E2M1X4 = mybir.dt.float4_e2m1fn_x4
 MULT = mybir.AluOpType.mult
 ADD = mybir.AluOpType.add
 
+COPY = mybir.ActivationFunctionType.Copy
+HEAD = 1024
+BLOCKS = HEAD // P
 GATHERS = (
-    (0, 0, 256), (0, 256, 832), (0, 832, 2176),
+    (0, HEAD, 2176),
     (1, 0, 1152), (2, 0, 2848), (3, 0, 3296),
     (1, 1152, 3584), (0, 2176, 4096), (2, 2848, 4096), (3, 3296, 4096), (1, 3584, 4096),
 )
@@ -49,7 +53,13 @@ def tile_moe_bdx_lin_none_kernel(tc, dyT, w_words, w_scales, gate, offs, pos1, p
         res1 = keep.tile([P, T], F32, name="res1")
         total = keep.tile([P, T], F32, name="total")
 
+        gate_col = keep.tile([P, BLOCKS], F32, name="gate_col")
+        head = keep.tile([P, HEAD], F32, name="head")
+        turned = keep.tile([P, BLOCKS, P], F32, name="turned")
+        ident = keep.tile([P, P], F32, name="ident")
+
         nc.gpsimd.memset(ws_sb[:].bitcast(I32), 0)
+        make_identity(nc, ident[:])
         for t in range(R):
             if widths[t] > T:
                 nc.gpsimd.memset(planes[t][:, T:], 0.0)
@@ -61,14 +71,15 @@ def tile_moe_bdx_lin_none_kernel(tc, dyT, w_words, w_scales, gate, offs, pos1, p
 
         nc.sync.dma_start(planes[0][:, :T], rows[:, 0, :])
         nc.sync.dma_start(offs_sb[:], offs)
-        loaded, have = {0}, 0
-        for t, a, b in GATHERS[:6]:
-            if b > have:
-                load_gate(have, b)
-                have = b
-            if t not in loaded:
-                nc.sync.dma_start(planes[t][:, :T], rows[:, t, :])
-                loaded.add(t)
+        have = GATHERS[0][2]
+        load_gate(HEAD, have)
+        nc.sync.dma_start(planes[1][:, :T], rows[:, 1, :])
+        load_gate(0, HEAD)
+        nc.sync.dma_start(gate_col[:], gate[0, 0:HEAD].rearrange("(p b) -> p b", b=BLOCKS))
+        for t, a, b in GATHERS[2:4]:
+            load_gate(have, b)
+            have = b
+            nc.sync.dma_start(planes[t][:, :T], rows[:, t, :])
         load_gate(have, SLOTS)
         nc.sync.dma_start(
             w_sb[:].bitcast(I32).rearrange("p (e n) -> p e n", e=E),
@@ -96,6 +107,24 @@ def tile_moe_bdx_lin_none_kernel(tc, dyT, w_words, w_scales, gate, offs, pos1, p
             )
 
         raw = keep.tile([P, R, SLOTS // 4, 4], F32, name="raw")
+        nc.vector.tensor_copy(head[:], planes[0][:].indirect(offs_sb[:, : HEAD // 16]))
+        by_block = head[:].rearrange("n (p b) -> n b p", b=BLOCKS)
+        for j in range(BLOCKS // 4):
+            acc = psum.tile([P, C], F32, name="acc")
+            for i in range(4):
+                nc.tensor.transpose(acc[:, i * P : (i + 1) * P], by_block[:, 4 * j + i, :], ident[:])
+            for i in range(4):
+                b = 4 * j + i
+                nc.scalar.activation(turned[:, b, :], acc[:, i * P : (i + 1) * P], COPY, scale=gate_col[:, b : b + 1])
+        for j in range(BLOCKS // 4):
+            acc = psum.tile([P, C], F32, name="acc")
+            for i in range(4):
+                nc.tensor.transpose(acc[:, i * P : (i + 1) * P], turned[:, 4 * j + i, :], ident[:])
+            nc.scalar.copy(
+                raw[:, 0, : HEAD // 4, :].rearrange("n (p j) i -> n j p i", j=BLOCKS // 4)[:, j, :, :],
+                acc[:].rearrange("n (i p) -> n p i", i=4),
+            )
+
         done = [0] * R
         for t, a, b in GATHERS:
             nc.vector.tensor_tensor(

@@ -26,9 +26,9 @@ COPY = mybir.ActivationFunctionType.Copy
 HEAD = 1024
 BLOCKS = HEAD // P
 GATHERS = (
-    (0, HEAD, 2176),
-    (1, 0, 1152), (2, 0, 2848), (3, 0, 3296),
-    (1, 1152, 3584), (0, 2176, 4096), (2, 2848, 4096), (3, 3296, 4096), (1, 3584, 4096),
+    (0, HEAD, 2240),
+    (1, 0, 1248), (2, 0, 2880), (3, 0, 3296),
+    (1, 1248, 3584), (0, 2240, 4096), (2, 2880, 4096), (3, 3296, 4096), (1, 3584, 4096),
 )
 QUANT = tuple((e * C, (e + 1) * C) for e in range(E - 1)) + ((3584, 3840), (3840, 4096))
 

@@ -165,8 +165,8 @@ def tile_moe_bdx_lin_none_kernel(tc, dyT, w_words, w_scales, gate, offs, pos1, p
         for engine_copy, (slots, sums) in zip((nc.scalar.copy, nc.vector.tensor_copy, nc.vector.tensor_copy, nc.scalar.copy), late):
             engine_copy(slots, sums)
 
-        for a, b in ((0, 1088), (1088, 2048)):
+        for a, b in ((0, 992), (992, 2048)):
             nc.vector.tensor_copy(res1[:, a:b], dx[:].indirect(pos1_sb[:, a // 16 : b // 16]))
-        for a, b in ((0, 1088), (1088, 1664), (1664, 1920), (1920, 2048)):
+        for a, b in ((0, 992), (992, 1568), (1568, 1920), (1920, 2048)):
             nc.vector.tensor_tensor(total[:, a:b], dx[:].indirect(pos2_sb[:, a // 16 : b // 16]), res1[:, a:b], ADD)
             nc.sync.dma_start(out[:, a:b], total[:, a:b])

@@ -54,15 +54,17 @@ def tile_moe_bdx_lin_none_kernel(tc, dyT, w_words, w_scales, gate, offs, pos1, p
         total = keep.tile([P, T], F32, name="total")
 
         gate_col = keep.tile([P, BLOCKS], F32, name="gate_col")
+        gate_rows = keep.tile([P, P], F32, name="gate_rows")
         head = keep.tile([P, HEAD], F32, name="head")
         turned = keep.tile([P, BLOCKS, P], F32, name="turned")
         ident = keep.tile([P, P], F32, name="ident")
 
-        nc.gpsimd.memset(ws_sb[:].bitcast(I32), 0)
+        nc.vector.memset(gate_rows[:], 0.0)
+        nc.vector.memset(ws_sb[:].bitcast(I32), 0)
         make_identity(nc, ident[:])
         for t in range(R):
             if widths[t] > T:
-                nc.gpsimd.memset(planes[t][:, T:], 0.0)
+                nc.vector.memset(planes[t][:, T:], 0.0)
 
         rows = dyT.rearrange("(p t) w -> p t w", t=R)
 
@@ -75,7 +77,7 @@ def tile_moe_bdx_lin_none_kernel(tc, dyT, w_words, w_scales, gate, offs, pos1, p
         load_gate(HEAD, have)
         nc.sync.dma_start(planes[1][:, :T], rows[:, 1, :])
         load_gate(0, HEAD)
-        nc.sync.dma_start(gate_col[:], gate[0, 0:HEAD].rearrange("(p b) -> p b", b=BLOCKS))
+        nc.sync.dma_start(gate_rows[:BLOCKS, :], gate[0, 0:HEAD].rearrange("(b p) -> b p", p=P))
         for t, a, b in GATHERS[2:4]:
             load_gate(have, b)
             have = b
@@ -108,7 +110,10 @@ def tile_moe_bdx_lin_none_kernel(tc, dyT, w_words, w_scales, gate, offs, pos1, p
 
         raw = keep.tile([P, R, SLOTS // 4, 4], F32, name="raw")
         nc.vector.tensor_copy(head[:], planes[0][:].indirect(offs_sb[:, : HEAD // 16]))
-        by_block = head[:].rearrange("n (p b) -> n b p", b=BLOCKS)
+        by_block = head[:].rearrange("n (b p) -> n b p", p=P)
+        acc = psum.tile([P, C], F32, name="acc")
+        nc.tensor.transpose(acc[:, :P], gate_rows[:], ident[:])
+        nc.scalar.copy(gate_col[:], acc[:, :BLOCKS])
         for j in range(BLOCKS // 4):
             acc = psum.tile([P, C], F32, name="acc")
             for i in range(4):
@@ -121,8 +126,8 @@ def tile_moe_bdx_lin_none_kernel(tc, dyT, w_words, w_scales, gate, offs, pos1, p
             for i in range(4):
                 nc.tensor.transpose(acc[:, i * P : (i + 1) * P], turned[:, 4 * j + i, :], ident[:])
             nc.scalar.copy(
-                raw[:, 0, : HEAD // 4, :].rearrange("n (p j) i -> n j p i", j=BLOCKS // 4)[:, j, :, :],
-                acc[:].rearrange("n (i p) -> n p i", i=4),
+                raw[:, 0, j * P : (j + 1) * P, :],
+                acc[:].rearrange("n (c i) -> n c i", i=4),
             )
 
         done = [0] * R

@@ -23,12 +23,11 @@ MULT = mybir.AluOpType.mult
 ADD = mybir.AluOpType.add
 
 COPY = mybir.ActivationFunctionType.Copy
-HEAD = 1024
+HEAD = 2048
 BLOCKS = HEAD // P
 GATHERS = (
-    (0, HEAD, 2240),
-    (1, 0, 1248), (2, 0, 2880), (3, 0, 3296),
-    (1, 1248, 3584), (0, 2240, 4096), (2, 2880, 4096), (3, 3296, 4096), (1, 3584, 4096),
+    (1, 0, 1216), (2, 0, 2784), (3, 0, 3232),
+    (1, 1216, 3520), (0, HEAD, 3712), (2, 2784, 4096), (3, 3232, 4096), (1, 3520, 4096), (0, 3712, 4096),
 )
 QUANT = tuple((e * C, (e + 1) * C) for e in range(E - 1)) + ((3584, 3840), (3840, 4096))
 
@@ -42,7 +41,7 @@ def tile_moe_bdx_lin_none_kernel(tc, dyT, w_words, w_scales, gate, offs, pos1, p
         offs_sb = keep.tile([P, SLOTS // 16], U16, name="offs_sb")
         pos1_sb = keep.tile([P, T // 16], U16, name="pos1_sb")
         pos2_sb = keep.tile([P, T // 16], U16, name="pos2_sb")
-        widths = [max(T, 32 + max(b - a for u, a, b in GATHERS if u == t)) for t in range(R)]
+        widths = [max(T, 32 + max(b - a for u, a, b in GATHERS + ((0, 0, HEAD),) if u == t)) for t in range(R)]
         planes = [keep.tile([P, widths[t]], F32, name=f"plane{t}") for t in range(R)]
         gate_sb = keep.tile([P, SLOTS], F32, name="gate_sb")
         w_sb = keep.tile([P, E * 2 * K], U8, name="w_sb", align_bytes=64)
@@ -74,11 +73,10 @@ def tile_moe_bdx_lin_none_kernel(tc, dyT, w_words, w_scales, gate, offs, pos1, p
         nc.sync.dma_start(planes[0][:, :T], rows[:, 0, :])
         nc.sync.dma_start(offs_sb[:], offs)
         have = GATHERS[0][2]
-        load_gate(HEAD, have)
         nc.sync.dma_start(planes[1][:, :T], rows[:, 1, :])
-        load_gate(0, HEAD)
+        load_gate(0, have)
         nc.sync.dma_start(gate_rows[:BLOCKS, :], gate[0, 0:HEAD].rearrange("(b p) -> b p", p=P))
-        for t, a, b in GATHERS[2:4]:
+        for t, a, b in GATHERS[1:3]:
             load_gate(have, b)
             have = b
             nc.sync.dma_start(planes[t][:, :T], rows[:, t, :])
@@ -95,14 +93,18 @@ def tile_moe_bdx_lin_none_kernel(tc, dyT, w_words, w_scales, gate, offs, pos1, p
         nc.sync.dma_start(pos1_sb[:], pos1)
         nc.sync.dma_start(pos2_sb[:], pos2)
 
-        grouped = keep.tile([P, SLOTS - C, R], BF16, name="grouped", align_bytes=64)
-        grouped_last = dx[:, (E - 3) * C : (E - 1) * C].bitcast(BF16).rearrange("p (c t) -> p c t", t=R)
+        base = SLOTS - C // 2
+        grouped = keep.tile([P, base, R], BF16, name="grouped", align_bytes=64)
+        grouped_last = dx[:, (E - 2) * C : (E - 1) * C].bitcast(BF16).rearrange("p (c t) -> p c t", t=R)
 
         def rounded(a, b):
-            base = SLOTS - C
             return grouped[:, a:b, :] if b <= base else grouped_last[:, a - base : b - base, :]
 
-        def interleave(raw, base, a, b):
+        def interleave(raw, a, b):
+            if a < base < b:
+                interleave(raw, a, base)
+                interleave(raw, base, b)
+                return
             nc.scalar.copy(
                 rounded(a, b).rearrange("p (c i) t -> p c t i", i=4),
                 raw[:, :, a // 4 : b // 4, :].rearrange("p t c i -> p c t i"),
@@ -114,23 +116,23 @@ def tile_moe_bdx_lin_none_kernel(tc, dyT, w_words, w_scales, gate, offs, pos1, p
         acc = psum.tile([P, C], F32, name="acc")
         nc.tensor.transpose(acc[:, :P], gate_rows[:], ident[:])
         nc.scalar.copy(gate_col[:], acc[:, :BLOCKS])
-        for j in range(BLOCKS // 4):
+        banks = [range(b, min(b + 4, BLOCKS)) for b in range(0, BLOCKS, 4)]
+        for blocks in banks:
             acc = psum.tile([P, C], F32, name="acc")
-            for i in range(4):
-                nc.tensor.transpose(acc[:, i * P : (i + 1) * P], by_block[:, 4 * j + i, :], ident[:])
-            for i in range(4):
-                b = 4 * j + i
+            for i, b in enumerate(blocks):
+                nc.tensor.transpose(acc[:, i * P : (i + 1) * P], by_block[:, b, :], ident[:])
+            for i, b in enumerate(blocks):
                 nc.scalar.activation(turned[:, b, :], acc[:, i * P : (i + 1) * P], COPY, scale=gate_col[:, b : b + 1])
-        for j in range(BLOCKS // 4):
+        for blocks in banks:
             acc = psum.tile([P, C], F32, name="acc")
-            for i in range(4):
-                nc.tensor.transpose(acc[:, i * P : (i + 1) * P], turned[:, 4 * j + i, :], ident[:])
+            for i, b in enumerate(blocks):
+                nc.tensor.transpose(acc[:, i * P : (i + 1) * P], turned[:, b, :], ident[:])
             nc.scalar.copy(
-                raw[:, 0, j * P : (j + 1) * P, :],
-                acc[:].rearrange("n (c i) -> n c i", i=4),
+                raw[:, 0, blocks[0] * P // 4 : (blocks[-1] + 1) * P // 4, :],
+                acc[:, : len(blocks) * P].rearrange("n (c i) -> n c i", i=4),
             )
 
-        done = [0] * R
+        done = [HEAD, 0, 0, 0]
         for t, a, b in GATHERS:
             nc.vector.tensor_tensor(
                 raw[:, t, a // 4 : b // 4, :],
@@ -141,7 +143,7 @@ def tile_moe_bdx_lin_none_kernel(tc, dyT, w_words, w_scales, gate, offs, pos1, p
             front = min(done)
             done[t] = b
             if min(done) > front:
-                interleave(raw, 0, front, min(done))
+                interleave(raw, front, min(done))
 
         late = []
         for a, b in QUANT:
@@ -163,11 +165,11 @@ def tile_moe_bdx_lin_none_kernel(tc, dyT, w_words, w_scales, gate, offs, pos1, p
                     start=True,
                     stop=True,
                 )
-                if e < E - 3:
+                if e < E - 2:
                     nc.scalar.copy(dx[:, lo:hi], acc[:])
                 else:
                     late.append((dx[:, lo:hi], acc[:, C - (hi - lo) : C]))
-        for engine_copy, (slots, sums) in zip((nc.scalar.copy, nc.vector.tensor_copy, nc.vector.tensor_copy, nc.scalar.copy), late):
+        for engine_copy, (slots, sums) in zip((nc.vector.tensor_copy, nc.scalar.copy, nc.scalar.copy), late):
             engine_copy(slots, sums)
 
         for a, b in ((0, 992), (992, 2048)):

@@ -61,9 +61,8 @@ def tile_moe_bdx_lin_none_kernel(tc, dyT, w_words, w_scales, gate, offs, pos1, p
         nc.vector.memset(gate_rows[:], 0.0)
         nc.vector.memset(ws_sb[:].bitcast(I32), 0)
         make_identity(nc, ident[:])
-        for t in range(R):
-            if widths[t] > T:
-                nc.vector.memset(planes[t][:, T:], 0.0)
+        for t, engine in enumerate((nc.vector, nc.vector, nc.gpsimd, nc.gpsimd)):
+            engine.memset(planes[t][:, T:], 0.0)
 
         rows = dyT.rearrange("(p t) w -> p t w", t=R)
 
@@ -172,8 +171,8 @@ def tile_moe_bdx_lin_none_kernel(tc, dyT, w_words, w_scales, gate, offs, pos1, p
         for engine_copy, (slots, sums) in zip((nc.vector.tensor_copy, nc.scalar.copy, nc.scalar.copy), late):
             engine_copy(slots, sums)
 
-        for a, b in ((0, 992), (992, 2048)):
+        for a, b in ((0, 1024), (1024, 2048)):
             nc.vector.tensor_copy(res1[:, a:b], dx[:].indirect(pos1_sb[:, a // 16 : b // 16]))
-        for a, b in ((0, 992), (992, 1568), (1568, 1920), (1920, 2048)):
+        for a, b in ((0, 1024), (1024, 1600), (1600, 1920), (1920, 2048)):
             nc.vector.tensor_tensor(total[:, a:b], dx[:].indirect(pos2_sb[:, a // 16 : b // 16]), res1[:, a:b], ADD)
             nc.sync.dma_start(out[:, a:b], total[:, a:b])

@@ -92,9 +92,9 @@ def tile_moe_bdx_lin_none_kernel(tc, dyT, w_words, w_scales, gate, offs, pos1, p
         nc.sync.dma_start(pos1_sb[:], pos1)
         nc.sync.dma_start(pos2_sb[:], pos2)
 
-        base = SLOTS - C // 2
+        base = SLOTS - C
         grouped = keep.tile([P, base, R], BF16, name="grouped", align_bytes=64)
-        grouped_last = dx[:, (E - 2) * C : (E - 1) * C].bitcast(BF16).rearrange("p (c t) -> p c t", t=R)
+        grouped_last = dx[:, (E - 2) * C :].bitcast(BF16).rearrange("p (c t) -> p c t", t=R)
 
         def rounded(a, b):
             return grouped[:, a:b, :] if b <= base else grouped_last[:, a - base : b - base, :]

@@ -93,7 +93,7 @@ def tile_moe_bdx_lin_none_kernel(tc, dyT, w_words, w_scales, gate, offs, pos1, p
         nc.sync.dma_start(pos2_sb[:], pos2)
 
         base = SLOTS - C
-        grouped = keep.tile([P, base, R], BF16, name="grouped", align_bytes=64)
+        grouped = keep.tile([P, base + 4, R], BF16, name="grouped", align_bytes=64)
         grouped_last = dx[:, (E - 2) * C :].bitcast(BF16).rearrange("p (c t) -> p c t", t=R)
 
         def rounded(a, b):

@@ -43,7 +43,7 @@ def tile_moe_bdx_lin_none_kernel(tc, dyT, w_words, w_scales, gate, offs, pos1, p
         pos2_sb = keep.tile([P, T // 16], U16, name="pos2_sb")
         widths = [max(T, 32 + max(b - a for u, a, b in GATHERS + ((0, 0, HEAD),) if u == t)) for t in range(R)]
         planes = [keep.tile([P, widths[t]], F32, name=f"plane{t}") for t in range(R)]
-        gate_sb = keep.tile([P, SLOTS], F32, name="gate_sb")
+        gate_sb = keep.tile([P, SLOTS], F32, name="gate_sb", align_bytes=256)
         w_sb = keep.tile([P, E * 2 * K], U8, name="w_sb", align_bytes=64)
         ws_sb = keep.tile([P, E * K], U8, name="ws_sb", align_bytes=64)
         dx = keep.tile([P, SLOTS], F32, name="dx", align_bytes=64)
@@ -93,7 +93,7 @@ def tile_moe_bdx_lin_none_kernel(tc, dyT, w_words, w_scales, gate, offs, pos1, p
         nc.sync.dma_start(pos2_sb[:], pos2)
 
         base = SLOTS - C
-        grouped = keep.tile([P, base + 4, R], BF16, name="grouped", align_bytes=64)
+        grouped = keep.tile([P, base + 4, R], BF16, name="grouped", align_bytes=256)
         grouped_last = dx[:, (E - 2) * C :].bitcast(BF16).rearrange("p (c t) -> p c t", t=R)
 
         def rounded(a, b):

@@ -1,7 +1,6 @@
 from contextlib import ExitStack
 
 import concourse.mybir as mybir
-from concourse.masks import make_identity
 
 FLOPS = 2 * 512 * 128 * 4096
 BYTES = 4 * 512 * 2048 + 8 * 128 * 256 + 8 * 16 * 128 + 4 * 4096 + 128 * 512 * 2 + 4 * 128 * 2048
@@ -21,15 +20,13 @@ E5M2X4 = mybir.dt.float8_e5m2_x4
 E2M1X4 = mybir.dt.float4_e2m1fn_x4
 MULT = mybir.AluOpType.mult
 ADD = mybir.AluOpType.add
-
 COPY = mybir.ActivationFunctionType.Copy
-HEAD = 2048
-BLOCKS = HEAD // P
-GATHERS = (
-    (1, 0, 1216), (2, 0, 2784), (3, 0, 3232),
-    (1, 1216, 3520), (0, HEAD, 3712), (2, 2784, 4096), (3, 3232, 4096), (1, 3520, 4096), (0, 3712, 4096),
-)
-QUANT = tuple((e * C, (e + 1) * C) for e in range(E - 1)) + ((3584, 3840), (3840, 4096))
+
+EARLY = 1920
+FUSED = 3200
+RUN = 4
+EARLY_CUTS = (0, 384, 896, 1408, EARLY)
+LATE_CUTS = (EARLY, 2176, 2624, 3072, FUSED)
 
 
 def tile_moe_bdx_lin_none_kernel(tc, dyT, w_words, w_scales, gate, offs, pos1, pos2, out):
@@ -41,8 +38,7 @@ def tile_moe_bdx_lin_none_kernel(tc, dyT, w_words, w_scales, gate, offs, pos1, p
         offs_sb = keep.tile([P, SLOTS // 16], U16, name="offs_sb")
         pos1_sb = keep.tile([P, T // 16], U16, name="pos1_sb")
         pos2_sb = keep.tile([P, T // 16], U16, name="pos2_sb")
-        widths = [max(T, 32 + max(b - a for u, a, b in GATHERS + ((0, 0, HEAD),) if u == t)) for t in range(R)]
-        planes = [keep.tile([P, widths[t]], F32, name=f"plane{t}") for t in range(R)]
+        planes = [keep.tile([P, T], F32, name=f"plane{t}", align_bytes=256) for t in range(R)]
         gate_sb = keep.tile([P, SLOTS], F32, name="gate_sb", align_bytes=256)
         w_sb = keep.tile([P, E * 2 * K], U8, name="w_sb", align_bytes=64)
         ws_sb = keep.tile([P, E * K], U8, name="ws_sb", align_bytes=64)
@@ -51,35 +47,22 @@ def tile_moe_bdx_lin_none_kernel(tc, dyT, w_words, w_scales, gate, offs, pos1, p
         scales = keep.tile([P, SLOTS], U8, name="scales", align_bytes=64)
         res1 = keep.tile([P, T], F32, name="res1")
         total = keep.tile([P, T], F32, name="total")
+        grouped = keep.tile([P, SLOTS, R], BF16, name="grouped", align_bytes=256)
+        late_width = FUSED - EARLY
+        fused_width = SLOTS - FUSED
+        early = keep.tile([P, R, EARLY // RUN, RUN], F32, name="early")
+        late = keep.tile([P, R, late_width // RUN, RUN], F32, name="late")
+        fused = late[:, 1:].rearrange("p t c i -> p (t c) i")[:, : R * fused_width // RUN, :].rearrange("p (t c) i -> p t c i", t=R)
 
-        gate_col = keep.tile([P, BLOCKS], F32, name="gate_col")
-        gate_rows = keep.tile([P, P], F32, name="gate_rows")
-        head = keep.tile([P, HEAD], F32, name="head")
-        turned = keep.tile([P, BLOCKS, P], F32, name="turned")
-        ident = keep.tile([P, P], F32, name="ident")
-
-        nc.vector.memset(gate_rows[:], 0.0)
         nc.vector.memset(ws_sb[:].bitcast(I32), 0)
-        make_identity(nc, ident[:])
-        for t, engine in enumerate((nc.vector, nc.vector, nc.gpsimd, nc.gpsimd)):
-            engine.memset(planes[t][:, T:], 0.0)
 
         rows = dyT.rearrange("(p t) w -> p t w", t=R)
-
-        def load_gate(a, b):
-            nc.sync.dma_start(gate_sb[:, a:b], gate[0:P, a:b])
-
-        nc.sync.dma_start(planes[0][:, :T], rows[:, 0, :])
+        nc.sync.dma_start(planes[0][:], rows[:, 0, :])
         nc.sync.dma_start(offs_sb[:], offs)
-        have = GATHERS[0][2]
-        nc.sync.dma_start(planes[1][:, :T], rows[:, 1, :])
-        load_gate(0, have)
-        nc.sync.dma_start(gate_rows[:BLOCKS, :], gate[0, 0:HEAD].rearrange("(b p) -> b p", p=P))
-        for t, a, b in GATHERS[1:3]:
-            load_gate(have, b)
-            have = b
-            nc.sync.dma_start(planes[t][:, :T], rows[:, t, :])
-        load_gate(have, SLOTS)
+        nc.sync.dma_start(gate_sb[:, FUSED:], gate[0:P, FUSED:])
+        for t in range(1, R):
+            nc.sync.dma_start(planes[t][:], rows[:, t, :])
+        nc.sync.dma_start(gate_sb[:, :FUSED], gate[0:P, :FUSED])
         nc.sync.dma_start(
             w_sb[:].bitcast(I32).rearrange("p (e n) -> p e n", e=E),
             w_words.bitcast(I32).rearrange("e a p n -> p (e a) n"),
@@ -92,87 +75,107 @@ def tile_moe_bdx_lin_none_kernel(tc, dyT, w_words, w_scales, gate, offs, pos1, p
         nc.sync.dma_start(pos1_sb[:], pos1)
         nc.sync.dma_start(pos2_sb[:], pos2)
 
-        base = SLOTS - C
-        grouped = keep.tile([P, base + 4, R], BF16, name="grouped", align_bytes=256)
-        grouped_last = dx[:, (E - 2) * C :].bitcast(BF16).rearrange("p (c t) -> p c t", t=R)
+        def part(raw, first, a, b):
+            return raw[:, :, (a - first) // RUN : (b - first) // RUN, :]
 
-        def rounded(a, b):
-            return grouped[:, a:b, :] if b <= base else grouped_last[:, a - base : b - base, :]
+        def looked_up(t, a, b):
+            return planes[t][:].indirect(offs_sb[:, a // 16 : b // 16])
 
-        def interleave(raw, a, b):
-            if a < base < b:
-                interleave(raw, a, base)
-                interleave(raw, base, b)
-                return
-            nc.scalar.copy(
-                rounded(a, b).rearrange("p (c i) t -> p c t i", i=4),
-                raw[:, :, a // 4 : b // 4, :].rearrange("p t c i -> p c t i"),
-            )
+        def woven(a, b):
+            return grouped[:, a:b, :].rearrange("p (c i) t -> p c t i", i=RUN)
 
-        raw = keep.tile([P, R, SLOTS // 4, 4], F32, name="raw")
-        nc.vector.tensor_copy(head[:], planes[0][:].indirect(offs_sb[:, : HEAD // 16]))
-        by_block = head[:].rearrange("n (b p) -> n b p", p=P)
-        acc = psum.tile([P, C], F32, name="acc")
-        nc.tensor.transpose(acc[:, :P], gate_rows[:], ident[:])
-        nc.scalar.copy(gate_col[:], acc[:, :BLOCKS])
-        banks = [range(b, min(b + 4, BLOCKS)) for b in range(0, BLOCKS, 4)]
-        for blocks in banks:
-            acc = psum.tile([P, C], F32, name="acc")
-            for i, b in enumerate(blocks):
-                nc.tensor.transpose(acc[:, i * P : (i + 1) * P], by_block[:, b, :], ident[:])
-            for i, b in enumerate(blocks):
-                nc.scalar.activation(turned[:, b, :], acc[:, i * P : (i + 1) * P], COPY, scale=gate_col[:, b : b + 1])
-        for blocks in banks:
-            acc = psum.tile([P, C], F32, name="acc")
-            for i, b in enumerate(blocks):
-                nc.tensor.transpose(acc[:, i * P : (i + 1) * P], turned[:, b, :], ident[:])
-            nc.scalar.copy(
-                raw[:, 0, blocks[0] * P // 4 : (blocks[-1] + 1) * P // 4, :],
-                acc[:, : len(blocks) * P].rearrange("n (c i) -> n c i", i=4),
-            )
+        def scalar_gather(raw, first, t, a, b):
+            nc.scalar.activation(part(raw, first, a, b)[:, t], looked_up(t, a, b), COPY)
 
-        done = [HEAD, 0, 0, 0]
-        for t, a, b in GATHERS:
+        def weigh(raw, first, a, b):
             nc.vector.tensor_tensor(
-                raw[:, t, a // 4 : b // 4, :],
-                planes[t][:].indirect(offs_sb[:, a // 16 : b // 16]),
-                gate_sb[:, a:b].rearrange("p (c i) -> p c i", i=4),
+                woven(a, b),
+                part(raw, first, a, b).rearrange("p t c i -> p c t i"),
+                gate_sb[:, a:b].rearrange("p (c i) -> p c i", i=RUN).unsqueeze(2).to_broadcast([P, (b - a) // RUN, R, RUN]),
                 MULT,
             )
-            front = min(done)
-            done[t] = b
-            if min(done) > front:
-                interleave(raw, front, min(done))
 
-        late = []
-        for a, b in QUANT:
+        def quantise(a, b):
             nc.vector.quantize_mx(
                 out=codes[:, a:b].bitcast(E5M2X4),
                 scales=scales[:, a:b],
-                in_=rounded(a, b).rearrange("p c t -> p (c t)"),
+                in_=grouped[:, a:b, :].rearrange("p c t -> p (c t)"),
             )
-            for lo in range(a, b, C):
-                hi = min(lo + C, b)
-                e = lo // C
-                acc = psum.tile([P, C], F32, name="acc")
+
+        banks = []
+
+        def multiply(*cuts):
+            e = cuts[0] // C
+            acc = psum.tile([P, C], F32, name="acc")
+            for a, b in zip(cuts, cuts[1:]):
                 nc.tensor.matmul_mx(
-                    out=acc[:],
+                    out=acc[:, a - cuts[0] : b - cuts[0]],
                     lhsT=w_sb[:, e * 2 * K : (e + 1) * 2 * K].bitcast(E2M1X4),
                     lhsT_scale=ws_sb[:, e * K : (e + 1) * K],
-                    rhs=codes[:, hi - C : hi].bitcast(E5M2X4),
-                    rhs_scale=scales[:, hi - C : hi],
+                    rhs=codes[:, a:b].bitcast(E5M2X4),
+                    rhs_scale=scales[:, a:b],
                     start=True,
                     stop=True,
                 )
-                if e < E - 2:
-                    nc.scalar.copy(dx[:, lo:hi], acc[:])
-                else:
-                    late.append((dx[:, lo:hi], acc[:, C - (hi - lo) : C]))
-        for engine_copy, (slots, sums) in zip((nc.vector.tensor_copy, nc.scalar.copy, nc.scalar.copy), late):
-            engine_copy(slots, sums)
+            nc.scalar.copy(dx[:, cuts[0] : cuts[-1]], acc[:, : cuts[-1] - cuts[0]])
 
-        for a, b in ((0, 1024), (1024, 2048)):
-            nc.vector.tensor_copy(res1[:, a:b], dx[:].indirect(pos1_sb[:, a // 16 : b // 16]))
-        for a, b in ((0, 1024), (1024, 1600), (1600, 1920), (1920, 2048)):
+        for t in range(R - 1):
+            scalar_gather(early, 0, t, 0, EARLY)
+        for a, b in zip(EARLY_CUTS, EARLY_CUTS[1:]):
+            scalar_gather(early, 0, R - 1, a, b)
+
+        nc.vector.tensor_copy(late[:, 0], looked_up(0, EARLY, FUSED))
+        middle = (E - 1) * C
+        for t, a, b in ((0, FUSED, SLOTS), (1, FUSED, SLOTS), (2, FUSED, SLOTS), (3, middle, SLOTS), (3, FUSED, middle)):
+            nc.vector.tensor_tensor(
+                part(fused, FUSED, a, b)[:, t],
+                looked_up(t, a, b),
+                gate_sb[:, a:b].rearrange("p (c i) -> p c i", i=RUN),
+                MULT,
+            )
+        for a, b in ((middle, SLOTS), (FUSED, middle)):
+            nc.vector.tensor_copy(woven(a, b), part(fused, FUSED, a, b).rearrange("p t c i -> p c t i"))
+
+        for t in range(1, R - 1):
+            scalar_gather(late, EARLY, t, EARLY, FUSED)
+        for a, b in zip(LATE_CUTS, LATE_CUTS[1:]):
+            scalar_gather(late, EARLY, R - 1, a, b)
+
+        quantise(middle, SLOTS)
+        multiply(middle, SLOTS)
+        quantise(3328, middle)
+        quantise(FUSED, 3328)
+        multiply(FUSED, 3328, middle)
+
+        weigh(early, 0, 0, 384)
+        weigh(early, 0, 384, 896)
+        weigh(early, 0, 896, 1408)
+        quantise(0, 512)
+        multiply(0, 512)
+        weigh(early, 0, 1408, EARLY)
+        quantise(512, 1024)
+        multiply(512, 1024)
+        quantise(1024, 1536)
+        multiply(1024, 1536)
+        weigh(late, EARLY, EARLY, 2176)
+        weigh(late, EARLY, 2176, 2624)
+        quantise(1536, 2048)
+        multiply(1536, 2048)
+        weigh(late, EARLY, 2624, 3072)
+        quantise(2048, 2560)
+        multiply(2048, 2560)
+        weigh(late, EARLY, 3072, FUSED)
+        quantise(2560, 3072)
+        multiply(2560, 3072)
+        quantise(3072, FUSED)
+        multiply(3072, FUSED)
+
+        nc.vector.tensor_copy(res1[:, 0:256], dx[:].indirect(pos1_sb[:, 0:16]))
+        for a, b in ((256, 512), (512, 1024), (1024, 1536), (1536, 2048)):
+            nc.scalar.activation(res1[:, a:b], dx[:].indirect(pos1_sb[:, a // 16 : b // 16]), COPY)
+        for a, b in ((256, 512), (0, 256), (512, 1024), (1024, 1536), (1536, 1920), (1920, 2048)):
             nc.vector.tensor_tensor(total[:, a:b], dx[:].indirect(pos2_sb[:, a // 16 : b // 16]), res1[:, a:b], ADD)
-            nc.sync.dma_start(out[:, a:b], total[:, a:b])
+            if a != 256:
+                lo = a
+                hi = 512 if a == 0 else b
+                nc.sync.dma_start(out[:, lo:hi], total[:, lo:hi])

@@ -22,11 +22,11 @@ MULT = mybir.AluOpType.mult
 ADD = mybir.AluOpType.add
 COPY = mybir.ActivationFunctionType.Copy
 
-EARLY = 1920
-FUSED = 3200
+EARLY = 2048
+SPARE = 32
+FUSED = 3072
+HEAD = 384
 RUN = 4
-EARLY_CUTS = (0, 384, 896, 1408, EARLY)
-LATE_CUTS = (EARLY, 2176, 2624, 3072, FUSED)
 
 
 def tile_moe_bdx_lin_none_kernel(tc, dyT, w_words, w_scales, gate, offs, pos1, pos2, out):
@@ -38,7 +38,8 @@ def tile_moe_bdx_lin_none_kernel(tc, dyT, w_words, w_scales, gate, offs, pos1, p
         offs_sb = keep.tile([P, SLOTS // 16], U16, name="offs_sb")
         pos1_sb = keep.tile([P, T // 16], U16, name="pos1_sb")
         pos2_sb = keep.tile([P, T // 16], U16, name="pos2_sb")
-        planes = [keep.tile([P, T], F32, name=f"plane{t}", align_bytes=256) for t in range(R)]
+        widths = (T, T + SPARE, T + SPARE, T)
+        planes = [keep.tile([P, widths[t]], F32, name=f"plane{t}", align_bytes=256) for t in range(R)]
         gate_sb = keep.tile([P, SLOTS], F32, name="gate_sb", align_bytes=256)
         w_sb = keep.tile([P, E * 2 * K], U8, name="w_sb", align_bytes=64)
         ws_sb = keep.tile([P, E * K], U8, name="ws_sb", align_bytes=64)
@@ -52,8 +53,10 @@ def tile_moe_bdx_lin_none_kernel(tc, dyT, w_words, w_scales, gate, offs, pos1, p
         fused_width = SLOTS - FUSED
         early = keep.tile([P, R, EARLY // RUN, RUN], F32, name="early")
         late = keep.tile([P, R, late_width // RUN, RUN], F32, name="late")
-        fused = late[:, 1:].rearrange("p t c i -> p (t c) i")[:, : R * fused_width // RUN, :].rearrange("p (t c) i -> p t c i", t=R)
+        fused = late[:, :, : fused_width // RUN, :]
 
+        nc.vector.memset(planes[1][:, T:], 0.0)
+        nc.scalar.copy(planes[2][:, T:], planes[1][:, T:])
         nc.vector.memset(ws_sb[:].bitcast(I32), 0)
 
         rows = dyT.rearrange("(p t) w -> p t w", t=R)
@@ -61,7 +64,7 @@ def tile_moe_bdx_lin_none_kernel(tc, dyT, w_words, w_scales, gate, offs, pos1, p
         nc.sync.dma_start(offs_sb[:], offs)
         nc.sync.dma_start(gate_sb[:, FUSED:], gate[0:P, FUSED:])
         for t in range(1, R):
-            nc.sync.dma_start(planes[t][:], rows[:, t, :])
+            nc.sync.dma_start(planes[t][:, :T], rows[:, t, :])
         nc.sync.dma_start(gate_sb[:, :FUSED], gate[0:P, :FUSED])
         nc.sync.dma_start(
             w_sb[:].bitcast(I32).rearrange("p (e n) -> p e n", e=E),
@@ -102,8 +105,6 @@ def tile_moe_bdx_lin_none_kernel(tc, dyT, w_words, w_scales, gate, offs, pos1, p
                 in_=grouped[:, a:b, :].rearrange("p c t -> p (c t)"),
             )
 
-        banks = []
-
         def multiply(*cuts):
             e = cuts[0] // C
             acc = psum.tile([P, C], F32, name="acc")
@@ -119,63 +120,57 @@ def tile_moe_bdx_lin_none_kernel(tc, dyT, w_words, w_scales, gate, offs, pos1, p
                 )
             nc.scalar.copy(dx[:, cuts[0] : cuts[-1]], acc[:, : cuts[-1] - cuts[0]])
 
-        for t in range(R - 1):
-            scalar_gather(early, 0, t, 0, EARLY)
-        for a, b in zip(EARLY_CUTS, EARLY_CUTS[1:]):
+        def product(a, b):
+            quantise(a, b)
+            for lo in range(a, b, C):
+                multiply(lo, min(lo + C, b))
+
+        scalar_gather(early, 0, 0, 0, EARLY - HEAD)
+        scalar_gather(early, 0, 1, 0, EARLY)
+        scalar_gather(early, 0, 2, 0, EARLY)
+        for a, b in ((0, 512), (512, 1152), (1152, EARLY)):
             scalar_gather(early, 0, R - 1, a, b)
 
-        nc.vector.tensor_copy(late[:, 0], looked_up(0, EARLY, FUSED))
+        nc.vector.tensor_copy(part(early, 0, EARLY - HEAD, EARLY)[:, 0], looked_up(0, EARLY - HEAD, EARLY))
         middle = (E - 1) * C
-        for t, a, b in ((0, FUSED, SLOTS), (1, FUSED, SLOTS), (2, FUSED, SLOTS), (3, middle, SLOTS), (3, FUSED, middle)):
+        for t, a, b in ((0, FUSED, SLOTS), (1, FUSED, SLOTS), (2, FUSED, SLOTS), (3, FUSED, middle), (3, middle, SLOTS)):
             nc.vector.tensor_tensor(
                 part(fused, FUSED, a, b)[:, t],
                 looked_up(t, a, b),
                 gate_sb[:, a:b].rearrange("p (c i) -> p c i", i=RUN),
                 MULT,
             )
-        for a, b in ((middle, SLOTS), (FUSED, middle)):
+        for a, b in ((FUSED, middle), (middle, SLOTS)):
             nc.vector.tensor_copy(woven(a, b), part(fused, FUSED, a, b).rearrange("p t c i -> p c t i"))
 
-        for t in range(1, R - 1):
-            scalar_gather(late, EARLY, t, EARLY, FUSED)
-        for a, b in zip(LATE_CUTS, LATE_CUTS[1:]):
-            scalar_gather(late, EARLY, R - 1, a, b)
+        half = 2560
+        for t, a, b in ((0, EARLY, FUSED), (1, EARLY, FUSED), (2, EARLY, half), (3, EARLY, half), (2, half, FUSED), (3, half, FUSED)):
+            scalar_gather(late, EARLY, t, a, b)
 
-        quantise(middle, SLOTS)
-        multiply(middle, SLOTS)
-        quantise(3328, middle)
-        quantise(FUSED, 3328)
-        multiply(FUSED, 3328, middle)
+        product(FUSED, SLOTS)
+        weigh(early, 0, 0, 512)
+        weigh(early, 0, 512, 1152)
+        weigh(early, 0, 1152, EARLY)
+        product(0, 1024)
+        weigh(late, EARLY, EARLY, half)
+        product(1024, 2048)
+        product(2048, 2560)
+        weigh(late, EARLY, half, 2816)
+        weigh(late, EARLY, 2816, FUSED)
+        product(2560, 2816)
+        product(2816, 3072)
 
-        weigh(early, 0, 0, 384)
-        weigh(early, 0, 384, 896)
-        weigh(early, 0, 896, 1408)
-        quantise(0, 512)
-        multiply(0, 512)
-        weigh(early, 0, 1408, EARLY)
-        quantise(512, 1024)
-        multiply(512, 1024)
-        quantise(1024, 1536)
-        multiply(1024, 1536)
-        weigh(late, EARLY, EARLY, 2176)
-        weigh(late, EARLY, 2176, 2624)
-        quantise(1536, 2048)
-        multiply(1536, 2048)
-        weigh(late, EARLY, 2624, 3072)
-        quantise(2048, 2560)
-        multiply(2048, 2560)
-        weigh(late, EARLY, 3072, FUSED)
-        quantise(2560, 3072)
-        multiply(2560, 3072)
-        quantise(3072, FUSED)
-        multiply(3072, FUSED)
+        def results(pos_sb, a, b):
+            return dx[:].indirect(pos_sb[:, a // 16 : b // 16])
 
-        nc.vector.tensor_copy(res1[:, 0:256], dx[:].indirect(pos1_sb[:, 0:16]))
-        for a, b in ((256, 512), (512, 1024), (1024, 1536), (1536, 2048)):
-            nc.scalar.activation(res1[:, a:b], dx[:].indirect(pos1_sb[:, a // 16 : b // 16]), COPY)
-        for a, b in ((256, 512), (0, 256), (512, 1024), (1024, 1536), (1536, 1920), (1920, 2048)):
-            nc.vector.tensor_tensor(total[:, a:b], dx[:].indirect(pos2_sb[:, a // 16 : b // 16]), res1[:, a:b], ADD)
-            if a != 256:
-                lo = a
-                hi = 512 if a == 0 else b
-                nc.sync.dma_start(out[:, lo:hi], total[:, lo:hi])
+        first, both = 320, 1792
+        nc.vector.tensor_copy(res1[:, :first], results(pos1_sb, 0, first))
+        for a, b in ((first, 576), (576, 1088), (1088, 1600), (1600, T)):
+            nc.scalar.activation(res1[:, a:b], results(pos1_sb, a, b), COPY)
+        nc.scalar.activation(total[:, both:], results(pos2_sb, both, T), COPY)
+        nc.vector.tensor_tensor(total[:, first:576], results(pos2_sb, first, 576), res1[:, first:576], ADD)
+        for a, b, end in ((0, first, 576), (576, 1088, 1088), (1088, 1600, 1600), (1600, both, both)):
+            nc.vector.tensor_tensor(total[:, a:b], results(pos2_sb, a, b), res1[:, a:b], ADD)
+            nc.sync.dma_start(out[:, a:end], total[:, a:end])
+        nc.vector.tensor_tensor(total[:, both:], total[:, both:], res1[:, both:], ADD)
+        nc.sync.dma_start(out[:, both:], total[:, both:])

@@ -1,6 +1,7 @@
 from contextlib import ExitStack
 
 import concourse.mybir as mybir
+from concourse.masks import make_identity
 
 FLOPS = 2 * 512 * 128 * 4096
 BYTES = 4 * 512 * 2048 + 8 * 128 * 256 + 8 * 16 * 128 + 4 * 4096 + 128 * 512 * 2 + 4 * 128 * 2048
@@ -22,10 +23,12 @@ MULT = mybir.AluOpType.mult
 ADD = mybir.AluOpType.add
 COPY = mybir.ActivationFunctionType.Copy
 
-EARLY = 2048
-SPARE = 32
-FUSED = 3072
-HEAD = 384
+EARLY = 1728
+LATE = 2048
+FUSED = 2944
+HEAD = 512
+ARRIVAL = (0, 2, 1, 3)
+MOVED = (2048, 2944, 3072)
 RUN = 4
 
 
@@ -33,39 +36,48 @@ def tile_moe_bdx_lin_none_kernel(tc, dyT, w_words, w_scales, gate, offs, pos1, p
     nc = tc.nc
     with ExitStack() as ctx:
         keep = ctx.enter_context(tc.tile_pool(name="keep", bufs=1))
-        psum = ctx.enter_context(tc.psum_pool(name="psum", bufs=8))
+        psum = ctx.enter_context(tc.psum_pool(name="psum", bufs=1))
 
         offs_sb = keep.tile([P, SLOTS // 16], U16, name="offs_sb")
         pos1_sb = keep.tile([P, T // 16], U16, name="pos1_sb")
         pos2_sb = keep.tile([P, T // 16], U16, name="pos2_sb")
-        widths = (T, T + SPARE, T + SPARE, T)
-        planes = [keep.tile([P, widths[t]], F32, name=f"plane{t}", align_bytes=256) for t in range(R)]
-        gate_sb = keep.tile([P, SLOTS], F32, name="gate_sb", align_bytes=256)
+        planes = [keep.tile([P, T], F32, name=f"plane{t}", tag=f"plane{t}", align_bytes=256) for t in range(R)]
         w_sb = keep.tile([P, E * 2 * K], U8, name="w_sb", align_bytes=64)
         ws_sb = keep.tile([P, E * K], U8, name="ws_sb", align_bytes=64)
-        dx = keep.tile([P, SLOTS], F32, name="dx", align_bytes=64)
         codes = keep.tile([P, SLOTS], U32, name="codes", align_bytes=64)
         scales = keep.tile([P, SLOTS], U8, name="scales", align_bytes=64)
         res1 = keep.tile([P, T], F32, name="res1")
         total = keep.tile([P, T], F32, name="total")
         grouped = keep.tile([P, SLOTS, R], BF16, name="grouped", align_bytes=256)
-        late_width = FUSED - EARLY
+        middle_width = LATE - EARLY
+        late_width = FUSED - LATE
         fused_width = SLOTS - FUSED
         early = keep.tile([P, R, EARLY // RUN, RUN], F32, name="early")
-        late = keep.tile([P, R, late_width // RUN, RUN], F32, name="late")
-        fused = late[:, :, : fused_width // RUN, :]
+        fused = keep.tile([P, R, fused_width // RUN, RUN], F32, name="fused")
+        late = fused[:, :, : late_width // RUN, :]
+        spot = keep.tile([P, middle_width - 32 + fused_width], F32, name="spot", align_bytes=256)
+        middle = spot[:, : R * middle_width].rearrange("p (t c i) -> p t c i", t=R, i=RUN)
+        gate_sb = spot[:, middle_width - 32 :]
+        zero = keep.tile([P, 1], F32, name="zero")
+        blocks = FUSED // P
+        gate_rows = keep.tile([P, P], F32, name="gate_rows")
+        gate_col = keep.tile([P, blocks], F32, name="gate_col")
+        ident = keep.tile([P, P], F32, name="ident")
+        banks = [psum.tile([P, C], F32, name=f"bank{e}") for e in range(E)]
 
-        nc.vector.memset(planes[1][:, T:], 0.0)
-        nc.scalar.copy(planes[2][:, T:], planes[1][:, T:])
+        nc.vector.memset(zero[:], 0.0)
+        nc.vector.memset(gate_rows[32:64, :], 0.0)
+        nc.scalar.copy(gate_rows[64:, :], zero[64:, :].to_broadcast([64, P]))
+        make_identity(nc, ident[:])
         nc.vector.memset(ws_sb[:].bitcast(I32), 0)
 
         rows = dyT.rearrange("(p t) w -> p t w", t=R)
+        nc.sync.dma_start(gate_rows[: SLOTS // P, :], gate[0, :].rearrange("(b p) -> b p", p=P))
         nc.sync.dma_start(planes[0][:], rows[:, 0, :])
         nc.sync.dma_start(offs_sb[:], offs)
-        nc.sync.dma_start(gate_sb[:, FUSED:], gate[0:P, FUSED:])
-        for t in range(1, R):
+        nc.sync.dma_start(gate_sb, gate[0:P, FUSED:])
+        for t in ARRIVAL[1:]:
             nc.sync.dma_start(planes[t][:, :T], rows[:, t, :])
-        nc.sync.dma_start(gate_sb[:, :FUSED], gate[0:P, :FUSED])
         nc.sync.dma_start(
             w_sb[:].bitcast(I32).rearrange("p (e n) -> p e n", e=E),
             w_words.bitcast(I32).rearrange("e a p n -> p (e a) n"),
@@ -84,8 +96,12 @@ def tile_moe_bdx_lin_none_kernel(tc, dyT, w_words, w_scales, gate, offs, pos1, p
         def looked_up(t, a, b):
             return planes[t][:].indirect(offs_sb[:, a // 16 : b // 16])
 
+        def rounded(a, b):
+            shift = MOVED[2] - MOVED[0] if MOVED[0] <= a < MOVED[1] else 0
+            return grouped[:, a + shift : b + shift, :]
+
         def woven(a, b):
-            return grouped[:, a:b, :].rearrange("p (c i) t -> p c t i", i=RUN)
+            return rounded(a, b).rearrange("p (c i) t -> p c t i", i=RUN)
 
         def scalar_gather(raw, first, t, a, b):
             nc.scalar.activation(part(raw, first, a, b)[:, t], looked_up(t, a, b), COPY)
@@ -94,7 +110,7 @@ def tile_moe_bdx_lin_none_kernel(tc, dyT, w_words, w_scales, gate, offs, pos1, p
             nc.vector.tensor_tensor(
                 woven(a, b),
                 part(raw, first, a, b).rearrange("p t c i -> p c t i"),
-                gate_sb[:, a:b].rearrange("p (c i) -> p c i", i=RUN).unsqueeze(2).to_broadcast([P, (b - a) // RUN, R, RUN]),
+                banks[a // C][:, a % C : a % C + b - a].rearrange("p (c i) -> p c i", i=RUN).unsqueeze(2).to_broadcast([P, (b - a) // RUN, R, RUN]),
                 MULT,
             )
 
@@ -102,63 +118,83 @@ def tile_moe_bdx_lin_none_kernel(tc, dyT, w_words, w_scales, gate, offs, pos1, p
             nc.vector.quantize_mx(
                 out=codes[:, a:b].bitcast(E5M2X4),
                 scales=scales[:, a:b],
-                in_=grouped[:, a:b, :].rearrange("p c t -> p (c t)"),
+                in_=rounded(a, b).rearrange("p c t -> p (c t)"),
             )
 
-        def multiply(*cuts):
-            e = cuts[0] // C
-            acc = psum.tile([P, C], F32, name="acc")
-            for a, b in zip(cuts, cuts[1:]):
-                nc.tensor.matmul_mx(
-                    out=acc[:, a - cuts[0] : b - cuts[0]],
-                    lhsT=w_sb[:, e * 2 * K : (e + 1) * 2 * K].bitcast(E2M1X4),
-                    lhsT_scale=ws_sb[:, e * K : (e + 1) * K],
-                    rhs=codes[:, a:b].bitcast(E5M2X4),
-                    rhs_scale=scales[:, a:b],
-                    start=True,
-                    stop=True,
-                )
-            nc.scalar.copy(dx[:, cuts[0] : cuts[-1]], acc[:, : cuts[-1] - cuts[0]])
+        def multiply(a, b, bank):
+            e = a // C
+            nc.tensor.matmul_mx(
+                out=bank[:, : b - a],
+                lhsT=w_sb[:, e * 2 * K : (e + 1) * 2 * K].bitcast(E2M1X4),
+                lhsT_scale=ws_sb[:, e * K : (e + 1) * K],
+                rhs=codes[:, a:b].bitcast(E5M2X4),
+                rhs_scale=scales[:, a:b],
+                start=True,
+                stop=True,
+            )
 
-        def product(a, b):
-            quantise(a, b)
-            for lo in range(a, b, C):
-                multiply(lo, min(lo + C, b))
+        def empty(a, b, bank):
+            nc.scalar.copy(dx[:, a:b], bank[:, : b - a])
 
-        scalar_gather(early, 0, 0, 0, EARLY - HEAD)
-        scalar_gather(early, 0, 1, 0, EARLY)
-        scalar_gather(early, 0, 2, 0, EARLY)
-        for a, b in ((0, 512), (512, 1152), (1152, EARLY)):
-            scalar_gather(early, 0, R - 1, a, b)
+        nc.tensor.transpose(banks[E - 1][:, :P], gate_rows[:], ident[:])
+        nc.scalar.copy(gate_col[:], banks[E - 1][:, :blocks])
+        for b in range(blocks):
+            at = b * P % C
+            nc.tensor.transpose(banks[b * P // C][:, at : at + P], gate_col[:, b : b + 1].to_broadcast([P, P]), ident[:])
+
+        scalar_gather(early, 0, ARRIVAL[0], 0, EARLY - HEAD)
+        scalar_gather(early, 0, ARRIVAL[1], 0, EARLY)
+        scalar_gather(early, 0, ARRIVAL[2], 0, EARLY)
+        for a, b in ((0, 256), (256, 512), (512, 1024), (1024, EARLY)):
+            scalar_gather(early, 0, ARRIVAL[3], a, b)
 
         nc.vector.tensor_copy(part(early, 0, EARLY - HEAD, EARLY)[:, 0], looked_up(0, EARLY - HEAD, EARLY))
-        middle = (E - 1) * C
-        for t, a, b in ((0, FUSED, SLOTS), (1, FUSED, SLOTS), (2, FUSED, SLOTS), (3, FUSED, middle), (3, middle, SLOTS)):
+        for t in ARRIVAL:
             nc.vector.tensor_tensor(
-                part(fused, FUSED, a, b)[:, t],
-                looked_up(t, a, b),
-                gate_sb[:, a:b].rearrange("p (c i) -> p c i", i=RUN),
+                fused[:, t],
+                looked_up(t, FUSED, SLOTS),
+                gate_sb.rearrange("p (c i) -> p c i", i=RUN),
                 MULT,
             )
-        for a, b in ((FUSED, middle), (middle, SLOTS)):
-            nc.vector.tensor_copy(woven(a, b), part(fused, FUSED, a, b).rearrange("p t c i -> p c t i"))
+        for a, b in ((FUSED, FUSED + late_width), (FUSED + late_width, SLOTS)):
+            nc.gpsimd.tensor_scalar(woven(a, b), part(fused, FUSED, a, b).rearrange("p t c i -> p c t i"), 1.0, 0.0, MULT, ADD)
 
-        half = 2560
-        for t, a, b in ((0, EARLY, FUSED), (1, EARLY, FUSED), (2, EARLY, half), (3, EARLY, half), (2, half, FUSED), (3, half, FUSED)):
-            scalar_gather(late, EARLY, t, a, b)
+        for t in ARRIVAL:
+            scalar_gather(middle, EARLY, t, EARLY, LATE)
+        for t in ARRIVAL[:2]:
+            scalar_gather(late, LATE, t, LATE, FUSED)
+        for a, b in ((LATE, 2560), (2560, FUSED)):
+            for t in ARRIVAL[2:]:
+                scalar_gather(late, LATE, t, a, b)
+        dx = keep.tile([P, SLOTS], F32, name="dx", tag="plane3", align_bytes=256)
 
-        product(FUSED, SLOTS)
-        weigh(early, 0, 0, 512)
-        weigh(early, 0, 512, 1152)
-        weigh(early, 0, 1152, EARLY)
-        product(0, 1024)
-        weigh(late, EARLY, EARLY, half)
-        product(1024, 2048)
-        product(2048, 2560)
-        weigh(late, EARLY, half, 2816)
-        weigh(late, EARLY, 2816, FUSED)
-        product(2560, 2816)
-        product(2816, 3072)
+        for a, b in ((0, 256), (256, 512), (512, 1024), (1024, 1536), (1536, EARLY)):
+            weigh(early, 0, a, b)
+        quantise(0, 1024)
+        multiply(0, 512, banks[0])
+        multiply(512, 1024, banks[1])
+        weigh(middle, EARLY, EARLY, LATE)
+        quantise(3072, SLOTS)
+        multiply(3072, 3584, banks[6])
+        multiply(3584, SLOTS, banks[7])
+        quantise(FUSED, 3072)
+        quantise(1024, 2048)
+        multiply(1024, 1536, banks[2])
+        multiply(1536, 2048, banks[3])
+        for e in (0, 1, 6, 7, 2, 3):
+            empty(e * C, (e + 1) * C, banks[e])
+        multiply(FUSED, 3072, banks[1])
+        empty(FUSED, 3072, banks[1])
+        weigh(late, LATE, 2048, 2560)
+        weigh(late, LATE, 2560, 2816)
+        quantise(2048, 2560)
+        multiply(2048, 2560, banks[4])
+        empty(2048, 2560, banks[4])
+        weigh(late, LATE, 2816, FUSED)
+        for a, b, bank in ((2560, 2816, 0), (2816, FUSED, 5)):
+            quantise(a, b)
+            multiply(a, b, banks[bank])
+            empty(a, b, banks[bank])
 
         def results(pos_sb, a, b):
             return dx[:].indirect(pos_sb[:, a // 16 : b // 16])

@@ -23,10 +23,11 @@ MULT = mybir.AluOpType.mult
 ADD = mybir.AluOpType.add
 COPY = mybir.ActivationFunctionType.Copy
 
-EARLY = 1728
+EARLY = 1792
 LATE = 2048
 FUSED = 2944
-HEAD = 512
+HEAD = 704
+SHARE = (2304, 2560)
 ARRIVAL = (0, 2, 1, 3)
 MOVED = (2048, 2944, 3072)
 RUN = 4
@@ -58,6 +59,7 @@ def tile_moe_bdx_lin_none_kernel(tc, dyT, w_words, w_scales, gate, offs, pos1, p
         spot = keep.tile([P, middle_width - 32 + fused_width], F32, name="spot", align_bytes=256)
         middle = spot[:, : R * middle_width].rearrange("p (t c i) -> p t c i", t=R, i=RUN)
         gate_sb = spot[:, middle_width - 32 :]
+        gate_share = keep.tile([P, SHARE[1] - SHARE[0]], F32, name="gate_share")
         zero = keep.tile([P, 1], F32, name="zero")
         blocks = FUSED // P
         gate_rows = keep.tile([P, P], F32, name="gate_rows")
@@ -78,6 +80,7 @@ def tile_moe_bdx_lin_none_kernel(tc, dyT, w_words, w_scales, gate, offs, pos1, p
         nc.sync.dma_start(gate_sb, gate[0:P, FUSED:])
         for t in ARRIVAL[1:]:
             nc.sync.dma_start(planes[t][:, :T], rows[:, t, :])
+        nc.sync.dma_start(gate_share[:], gate[0:P, SHARE[0] : SHARE[1]])
         nc.sync.dma_start(
             w_sb[:].bitcast(I32).rearrange("p (e n) -> p e n", e=E),
             w_words.bitcast(I32).rearrange("e a p n -> p (e a) n"),
@@ -107,10 +110,14 @@ def tile_moe_bdx_lin_none_kernel(tc, dyT, w_words, w_scales, gate, offs, pos1, p
             nc.scalar.activation(part(raw, first, a, b)[:, t], looked_up(t, a, b), COPY)
 
         def weigh(raw, first, a, b):
-            nc.vector.tensor_tensor(
+            if (a, b) == SHARE:
+                engine, weights = nc.gpsimd, gate_share[:]
+            else:
+                engine, weights = nc.vector, banks[a // C][:, a % C : a % C + b - a]
+            engine.tensor_tensor(
                 woven(a, b),
                 part(raw, first, a, b).rearrange("p t c i -> p c t i"),
-                banks[a // C][:, a % C : a % C + b - a].rearrange("p (c i) -> p c i", i=RUN).unsqueeze(2).to_broadcast([P, (b - a) // RUN, R, RUN]),
+                weights.rearrange("p (c i) -> p c i", i=RUN).unsqueeze(2).to_broadcast([P, (b - a) // RUN, R, RUN]),
                 MULT,
             )
 
@@ -133,19 +140,21 @@ def tile_moe_bdx_lin_none_kernel(tc, dyT, w_words, w_scales, gate, offs, pos1, p
                 stop=True,
             )
 
-        def empty(a, b, bank):
-            nc.scalar.copy(dx[:, a:b], bank[:, : b - a])
+        def empty(a, b, bank, copy=nc.scalar.copy):
+            copy(dx[:, a:b], bank[:, : b - a])
 
         nc.tensor.transpose(banks[E - 1][:, :P], gate_rows[:], ident[:])
         nc.scalar.copy(gate_col[:], banks[E - 1][:, :blocks])
         for b in range(blocks):
+            if SHARE[0] <= b * P < SHARE[1]:
+                continue
             at = b * P % C
             nc.tensor.transpose(banks[b * P // C][:, at : at + P], gate_col[:, b : b + 1].to_broadcast([P, P]), ident[:])
 
         scalar_gather(early, 0, ARRIVAL[0], 0, EARLY - HEAD)
         scalar_gather(early, 0, ARRIVAL[1], 0, EARLY)
         scalar_gather(early, 0, ARRIVAL[2], 0, EARLY)
-        for a, b in ((0, 256), (256, 512), (512, 1024), (1024, EARLY)):
+        for a, b in ((0, 512), (512, 1152), (1152, EARLY)):
             scalar_gather(early, 0, ARRIVAL[3], a, b)
 
         nc.vector.tensor_copy(part(early, 0, EARLY - HEAD, EARLY)[:, 0], looked_up(0, EARLY - HEAD, EARLY))
@@ -156,45 +165,47 @@ def tile_moe_bdx_lin_none_kernel(tc, dyT, w_words, w_scales, gate, offs, pos1, p
                 gate_sb.rearrange("p (c i) -> p c i", i=RUN),
                 MULT,
             )
-        for a, b in ((FUSED, FUSED + late_width), (FUSED + late_width, SLOTS)):
+        for a, b in ((FUSED, FUSED + 512), (FUSED + 512, FUSED + late_width), (FUSED + late_width, SLOTS)):
             nc.gpsimd.tensor_scalar(woven(a, b), part(fused, FUSED, a, b).rearrange("p t c i -> p c t i"), 1.0, 0.0, MULT, ADD)
 
         for t in ARRIVAL:
             scalar_gather(middle, EARLY, t, EARLY, LATE)
-        for t in ARRIVAL[:2]:
-            scalar_gather(late, LATE, t, LATE, FUSED)
-        for a, b in ((LATE, 2560), (2560, FUSED)):
-            for t in ARRIVAL[2:]:
-                scalar_gather(late, LATE, t, a, b)
+        for t in ARRIVAL:
+            scalar_gather(late, LATE, t, LATE, 2560)
+        for t in ARRIVAL[:3]:
+            scalar_gather(late, LATE, t, 2560, FUSED)
+        for a, b in ((2560, 2816), (2816, FUSED)):
+            scalar_gather(late, LATE, ARRIVAL[3], a, b)
         dx = keep.tile([P, SLOTS], F32, name="dx", tag="plane3", align_bytes=256)
 
-        for a, b in ((0, 256), (256, 512), (512, 1024), (1024, 1536), (1536, EARLY)):
+        for a, b in ((0, 512), (512, 1024), (1024, 1536), (1536, EARLY)):
             weigh(early, 0, a, b)
+        weigh(middle, EARLY, EARLY, LATE)
         quantise(0, 1024)
         multiply(0, 512, banks[0])
         multiply(512, 1024, banks[1])
-        weigh(middle, EARLY, EARLY, LATE)
-        quantise(3072, SLOTS)
-        multiply(3072, 3584, banks[6])
-        multiply(3584, SLOTS, banks[7])
-        quantise(FUSED, 3072)
         quantise(1024, 2048)
         multiply(1024, 1536, banks[2])
         multiply(1536, 2048, banks[3])
-        for e in (0, 1, 6, 7, 2, 3):
+        quantise(FUSED, 3072)
+        quantise(3072, SLOTS)
+        multiply(3072, 3584, banks[6])
+        multiply(3584, SLOTS, banks[7])
+        for e in (0, 1, 2, 3, 6, 7):
             empty(e * C, (e + 1) * C, banks[e])
         multiply(FUSED, 3072, banks[1])
         empty(FUSED, 3072, banks[1])
-        weigh(late, LATE, 2048, 2560)
+        weigh(late, LATE, *SHARE)
+        weigh(late, LATE, 2048, 2304)
         weigh(late, LATE, 2560, 2816)
-        quantise(2048, 2560)
-        multiply(2048, 2560, banks[4])
-        empty(2048, 2560, banks[4])
         weigh(late, LATE, 2816, FUSED)
-        for a, b, bank in ((2560, 2816, 0), (2816, FUSED, 5)):
+        for a, b, bank in ((2048, 2304, 4), (2304, 2560, 2), (2560, 2816, 0), (2816, FUSED, 5)):
             quantise(a, b)
             multiply(a, b, banks[bank])
-            empty(a, b, banks[bank])
+        empty(2048, 2304, banks[4], nc.vector.tensor_copy)
+        empty(2304, 2560, banks[2])
+        empty(2560, 2816, banks[0], nc.vector.tensor_copy)
+        empty(2816, FUSED, banks[5])
 
         def results(pos_sb, a, b):
             return dx[:].indirect(pos_sb[:, a // 16 : b // 16])

@@ -23,13 +23,13 @@ MULT = mybir.AluOpType.mult
 ADD = mybir.AluOpType.add
 COPY = mybir.ActivationFunctionType.Copy
 
-EARLY = 1792
+EARLY = 1664
 LATE = 2048
-FUSED = 2944
-HEAD = 704
+FUSED = 2816
+HEAD = 320
 SHARE = (2304, 2560)
-ARRIVAL = (0, 2, 1, 3)
-MOVED = (2048, 2944, 3072)
+ARRIVAL = (0, 1, 2, 3)
+MOVED = (2048, 2816, 3072)
 RUN = 4
 
 
@@ -56,9 +56,9 @@ def tile_moe_bdx_lin_none_kernel(tc, dyT, w_words, w_scales, gate, offs, pos1, p
         early = keep.tile([P, R, EARLY // RUN, RUN], F32, name="early")
         fused = keep.tile([P, R, fused_width // RUN, RUN], F32, name="fused")
         late = fused[:, :, : late_width // RUN, :]
-        spot = keep.tile([P, middle_width - 32 + fused_width], F32, name="spot", align_bytes=256)
+        spot = keep.tile([P, middle_width + fused_width], F32, name="spot", align_bytes=256)
         middle = spot[:, : R * middle_width].rearrange("p (t c i) -> p t c i", t=R, i=RUN)
-        gate_sb = spot[:, middle_width - 32 :]
+        gate_sb = spot[:, middle_width:]
         gate_share = keep.tile([P, SHARE[1] - SHARE[0]], F32, name="gate_share")
         zero = keep.tile([P, 1], F32, name="zero")
         blocks = FUSED // P
@@ -77,7 +77,9 @@ def tile_moe_bdx_lin_none_kernel(tc, dyT, w_words, w_scales, gate, offs, pos1, p
         nc.sync.dma_start(gate_rows[: SLOTS // P, :], gate[0, :].rearrange("(b p) -> b p", p=P))
         nc.sync.dma_start(planes[0][:], rows[:, 0, :])
         nc.sync.dma_start(offs_sb[:], offs)
-        nc.sync.dma_start(gate_sb, gate[0:P, FUSED:])
+        cut = FUSED + fused_width // 2
+        for a, b in ((FUSED, cut), (cut, SLOTS)):
+            nc.sync.dma_start(gate_sb[:, a - FUSED : b - FUSED], gate[0:P, a:b])
         for t in ARRIVAL[1:]:
             nc.sync.dma_start(planes[t][:, :T], rows[:, t, :])
         nc.sync.dma_start(gate_share[:], gate[0:P, SHARE[0] : SHARE[1]])
@@ -152,31 +154,28 @@ def tile_moe_bdx_lin_none_kernel(tc, dyT, w_words, w_scales, gate, offs, pos1, p
             nc.tensor.transpose(banks[b * P // C][:, at : at + P], gate_col[:, b : b + 1].to_broadcast([P, P]), ident[:])
 
         scalar_gather(early, 0, ARRIVAL[0], 0, EARLY - HEAD)
+        scalar_gather(middle, EARLY, ARRIVAL[0], EARLY, LATE)
         scalar_gather(early, 0, ARRIVAL[1], 0, EARLY)
         scalar_gather(early, 0, ARRIVAL[2], 0, EARLY)
         for a, b in ((0, 512), (512, 1152), (1152, EARLY)):
             scalar_gather(early, 0, ARRIVAL[3], a, b)
 
         nc.vector.tensor_copy(part(early, 0, EARLY - HEAD, EARLY)[:, 0], looked_up(0, EARLY - HEAD, EARLY))
-        for t in ARRIVAL:
+        for t, a, b in ((0, FUSED, cut), (0, cut, SLOTS), (1, FUSED, SLOTS), (2, FUSED, SLOTS), (3, FUSED, SLOTS)):
             nc.vector.tensor_tensor(
-                fused[:, t],
-                looked_up(t, FUSED, SLOTS),
-                gate_sb.rearrange("p (c i) -> p c i", i=RUN),
+                part(fused, FUSED, a, b)[:, t],
+                looked_up(t, a, b),
+                gate_sb[:, a - FUSED : b - FUSED].rearrange("p (c i) -> p c i", i=RUN),
                 MULT,
             )
-        for a, b in ((FUSED, FUSED + 512), (FUSED + 512, FUSED + late_width), (FUSED + late_width, SLOTS)):
+        for a, b in ((FUSED, FUSED + late_width), (FUSED + late_width, SLOTS)):
             nc.gpsimd.tensor_scalar(woven(a, b), part(fused, FUSED, a, b).rearrange("p t c i -> p c t i"), 1.0, 0.0, MULT, ADD)
 
-        for t in ARRIVAL:
+        for t in ARRIVAL[1:]:
             scalar_gather(middle, EARLY, t, EARLY, LATE)
         for t in ARRIVAL:
-            scalar_gather(late, LATE, t, LATE, 2560)
-        for t in ARRIVAL[:3]:
-            scalar_gather(late, LATE, t, 2560, FUSED)
-        for a, b in ((2560, 2816), (2816, FUSED)):
-            scalar_gather(late, LATE, ARRIVAL[3], a, b)
-        dx = keep.tile([P, SLOTS], F32, name="dx", tag="plane3", align_bytes=256)
+            scalar_gather(late, LATE, t, LATE, FUSED)
+        dx = keep.tile([P, SLOTS], F32, name="dx", tag=f"plane{ARRIVAL[3]}", align_bytes=256)
 
         for a, b in ((0, 512), (512, 1024), (1024, 1536), (1536, EARLY)):
             weigh(early, 0, a, b)
@@ -189,23 +188,22 @@ def tile_moe_bdx_lin_none_kernel(tc, dyT, w_words, w_scales, gate, offs, pos1, p
         multiply(1536, 2048, banks[3])
         quantise(FUSED, 3072)
         quantise(3072, SLOTS)
-        multiply(3072, 3584, banks[6])
-        multiply(3584, SLOTS, banks[7])
-        for e in (0, 1, 2, 3, 6, 7):
+        multiply(FUSED, 3072, banks[6])
+        for e in range(4):
             empty(e * C, (e + 1) * C, banks[e])
-        multiply(FUSED, 3072, banks[1])
-        empty(FUSED, 3072, banks[1])
+        empty(FUSED, 3072, banks[6])
+        for e in (6, 7):
+            multiply(e * C, (e + 1) * C, banks[e - 6])
+            empty(e * C, (e + 1) * C, banks[e - 6])
         weigh(late, LATE, *SHARE)
         weigh(late, LATE, 2048, 2304)
         weigh(late, LATE, 2560, 2816)
-        weigh(late, LATE, 2816, FUSED)
-        for a, b, bank in ((2048, 2304, 4), (2304, 2560, 2), (2560, 2816, 0), (2816, FUSED, 5)):
+        for a, b, bank in ((2048, 2304, 4), (2560, 2816, 5), (2304, 2560, 2)):
             quantise(a, b)
             multiply(a, b, banks[bank])
-        empty(2048, 2304, banks[4], nc.vector.tensor_copy)
-        empty(2304, 2560, banks[2])
-        empty(2560, 2816, banks[0], nc.vector.tensor_copy)
-        empty(2816, FUSED, banks[5])
+        empty(2048, 2304, banks[4])
+        empty(2560, 2816, banks[5])
+        empty(2304, 2560, banks[2], nc.vector.tensor_copy)
 
         def results(pos_sb, a, b):
             return dx[:].indirect(pos_sb[:, a // 16 : b // 16])

@@ -7,9 +7,10 @@ FLOPS = 2 * 512 * 128 * 4096
 BYTES = 4 * 512 * 2048 + 8 * 128 * 256 + 8 * 16 * 128 + 4 * 4096 + 128 * 512 * 2 + 4 * 128 * 2048
 
 P = 128
-T, E, C, N, K = 2048, 8, 512, 512, 128
+T, E, C, K = 2048, 8, 512, 128
 SLOTS = E * C
 R = 4
+RUN = 4
 
 F32 = mybir.dt.float32
 BF16 = mybir.dt.bfloat16
@@ -23,14 +24,18 @@ MULT = mybir.AluOpType.mult
 ADD = mybir.AluOpType.add
 COPY = mybir.ActivationFunctionType.Copy
 
-EARLY = 1664
-LATE = 2048
-FUSED = 2816
-HEAD = 320
-SHARE = (2304, 2560)
-ARRIVAL = (0, 1, 2, 3)
-MOVED = (2048, 2816, 3072)
-RUN = 4
+MIDDLE = 3 * C
+LATE = 4 * C
+FUSED = 5 * C + C // 2
+HEAD = 416
+SHARE = (LATE + 320, LATE + C)
+FIRST = 320
+BOTH = 1792
+AHEAD = (FIRST, FIRST + 256, FIRST + 256 + C, FIRST + 256 + 2 * C, T)
+
+
+def pieces(*cuts):
+    return tuple(zip(cuts, cuts[1:]))
 
 
 def tile_moe_bdx_lin_none_kernel(tc, dyT, w_words, w_scales, gate, offs, pos1, pos2, out):
@@ -50,22 +55,21 @@ def tile_moe_bdx_lin_none_kernel(tc, dyT, w_words, w_scales, gate, offs, pos1, p
         res1 = keep.tile([P, T], F32, name="res1")
         total = keep.tile([P, T], F32, name="total")
         grouped = keep.tile([P, SLOTS, R], BF16, name="grouped", align_bytes=256)
-        middle_width = LATE - EARLY
-        late_width = FUSED - LATE
-        fused_width = SLOTS - FUSED
-        early = keep.tile([P, R, EARLY // RUN, RUN], F32, name="early")
+
+        middle_width, late_width, fused_width = LATE - MIDDLE, FUSED - LATE, SLOTS - FUSED
+        early = keep.tile([P, R, MIDDLE // RUN, RUN], F32, name="early")
         fused = keep.tile([P, R, fused_width // RUN, RUN], F32, name="fused")
         late = fused[:, :, : late_width // RUN, :]
-        spot = keep.tile([P, middle_width + fused_width], F32, name="spot", align_bytes=256)
-        middle = spot[:, : R * middle_width].rearrange("p (t c i) -> p t c i", t=R, i=RUN)
-        gate_sb = spot[:, middle_width:]
+        middle_flat = keep.tile([P, R * middle_width], F32, name="middle_flat", align_bytes=256)
+        middle = middle_flat[:].rearrange("p (t c i) -> p t c i", t=R, i=RUN)
+        gate_fused = middle_flat[:, middle_width : middle_width + fused_width]
         gate_share = keep.tile([P, SHARE[1] - SHARE[0]], F32, name="gate_share")
         zero = keep.tile([P, 1], F32, name="zero")
         blocks = FUSED // P
         gate_rows = keep.tile([P, P], F32, name="gate_rows")
         gate_col = keep.tile([P, blocks], F32, name="gate_col")
         ident = keep.tile([P, P], F32, name="ident")
-        banks = [psum.tile([P, C], F32, name=f"bank{e}") for e in range(E)]
+        banks = [psum.tile([P, C], F32, name=f"bank{b}") for b in range(E)]
 
         nc.vector.memset(zero[:], 0.0)
         nc.vector.memset(gate_rows[32:64, :], 0.0)
@@ -74,14 +78,14 @@ def tile_moe_bdx_lin_none_kernel(tc, dyT, w_words, w_scales, gate, offs, pos1, p
         nc.vector.memset(ws_sb[:].bitcast(I32), 0)
 
         rows = dyT.rearrange("(p t) w -> p t w", t=R)
-        nc.sync.dma_start(gate_rows[: SLOTS // P, :], gate[0, :].rearrange("(b p) -> b p", p=P))
+        half = FUSED + fused_width // 2
+        nc.scalar.dma_start(gate_rows[: SLOTS // P, :], gate[0, :].rearrange("(b p) -> b p", p=P))
         nc.sync.dma_start(planes[0][:], rows[:, 0, :])
         nc.sync.dma_start(offs_sb[:], offs)
-        cut = FUSED + fused_width // 2
-        for a, b in ((FUSED, cut), (cut, SLOTS)):
-            nc.sync.dma_start(gate_sb[:, a - FUSED : b - FUSED], gate[0:P, a:b])
-        for t in ARRIVAL[1:]:
-            nc.sync.dma_start(planes[t][:, :T], rows[:, t, :])
+        for a, b in pieces(FUSED, half, SLOTS):
+            nc.sync.dma_start(gate_fused[:, a - FUSED : b - FUSED], gate[0:P, a:b])
+        for t in range(1, R):
+            nc.sync.dma_start(planes[t][:], rows[:, t, :])
         nc.sync.dma_start(gate_share[:], gate[0:P, SHARE[0] : SHARE[1]])
         nc.sync.dma_start(
             w_sb[:].bitcast(I32).rearrange("p (e n) -> p e n", e=E),
@@ -95,33 +99,32 @@ def tile_moe_bdx_lin_none_kernel(tc, dyT, w_words, w_scales, gate, offs, pos1, p
         nc.sync.dma_start(pos1_sb[:], pos1)
         nc.sync.dma_start(pos2_sb[:], pos2)
 
-        def part(raw, first, a, b):
-            return raw[:, :, (a - first) // RUN : (b - first) // RUN, :]
+        def gathered(a, b):
+            region, first = [(r, f) for r, f in ((early, 0), (middle, MIDDLE), (late, LATE), (fused, FUSED)) if f <= a][-1]
+            return region[:, :, (a - first) // RUN : (b - first) // RUN, :]
 
         def looked_up(t, a, b):
             return planes[t][:].indirect(offs_sb[:, a // 16 : b // 16])
 
         def rounded(a, b):
-            shift = MOVED[2] - MOVED[0] if MOVED[0] <= a < MOVED[1] else 0
+            shift = 2 * C if LATE <= a < FUSED else 0
             return grouped[:, a + shift : b + shift, :]
 
         def woven(a, b):
             return rounded(a, b).rearrange("p (c i) t -> p c t i", i=RUN)
 
-        def scalar_gather(raw, first, t, a, b):
-            nc.scalar.activation(part(raw, first, a, b)[:, t], looked_up(t, a, b), COPY)
+        def by_runs(a, b):
+            return gathered(a, b).rearrange("p t c i -> p c t i")
 
-        def weigh(raw, first, a, b):
-            if (a, b) == SHARE:
-                engine, weights = nc.gpsimd, gate_share[:]
-            else:
-                engine, weights = nc.vector, banks[a // C][:, a % C : a % C + b - a]
-            engine.tensor_tensor(
-                woven(a, b),
-                part(raw, first, a, b).rearrange("p t c i -> p c t i"),
-                weights.rearrange("p (c i) -> p c i", i=RUN).unsqueeze(2).to_broadcast([P, (b - a) // RUN, R, RUN]),
-                MULT,
-            )
+        def scalar_gather(t, a, b):
+            nc.scalar.activation(gathered(a, b)[:, t], looked_up(t, a, b), COPY)
+
+        def weigh(engine, a, b, weights):
+            spread = weights.rearrange("p (c i) -> p c i", i=RUN).unsqueeze(2).to_broadcast([P, (b - a) // RUN, R, RUN])
+            engine.tensor_tensor(woven(a, b), by_runs(a, b), spread, MULT)
+
+        def vector_weigh(a, b):
+            weigh(nc.vector, a, b, banks[a // C][:, a % C : a % C + b - a])
 
         def quantise(a, b):
             nc.vector.quantize_mx(
@@ -142,80 +145,85 @@ def tile_moe_bdx_lin_none_kernel(tc, dyT, w_words, w_scales, gate, offs, pos1, p
                 stop=True,
             )
 
-        def empty(a, b, bank, copy=nc.scalar.copy):
+        def empty(copy, a, b, bank):
             copy(dx[:, a:b], bank[:, : b - a])
 
         nc.tensor.transpose(banks[E - 1][:, :P], gate_rows[:], ident[:])
         nc.scalar.copy(gate_col[:], banks[E - 1][:, :blocks])
         for b in range(blocks):
-            if SHARE[0] <= b * P < SHARE[1]:
-                continue
-            at = b * P % C
-            nc.tensor.transpose(banks[b * P // C][:, at : at + P], gate_col[:, b : b + 1].to_broadcast([P, P]), ident[:])
+            if not SHARE[0] <= b * P < SHARE[1]:
+                at = b * P % C
+                nc.tensor.transpose(banks[b * P // C][:, at : at + P], gate_col[:, b : b + 1].to_broadcast([P, P]), ident[:])
 
-        scalar_gather(early, 0, ARRIVAL[0], 0, EARLY - HEAD)
-        scalar_gather(middle, EARLY, ARRIVAL[0], EARLY, LATE)
-        scalar_gather(early, 0, ARRIVAL[1], 0, EARLY)
-        scalar_gather(early, 0, ARRIVAL[2], 0, EARLY)
-        for a, b in ((0, 512), (512, 1152), (1152, EARLY)):
-            scalar_gather(early, 0, ARRIVAL[3], a, b)
+        scalar_gather(0, 0, MIDDLE - HEAD)
+        scalar_gather(0, MIDDLE, LATE)
+        scalar_gather(1, 0, MIDDLE)
+        scalar_gather(2, 0, MIDDLE)
+        for a in range(0, MIDDLE, C):
+            scalar_gather(3, a, a + C)
 
-        nc.vector.tensor_copy(part(early, 0, EARLY - HEAD, EARLY)[:, 0], looked_up(0, EARLY - HEAD, EARLY))
-        for t, a, b in ((0, FUSED, cut), (0, cut, SLOTS), (1, FUSED, SLOTS), (2, FUSED, SLOTS), (3, FUSED, SLOTS)):
-            nc.vector.tensor_tensor(
-                part(fused, FUSED, a, b)[:, t],
-                looked_up(t, a, b),
-                gate_sb[:, a - FUSED : b - FUSED].rearrange("p (c i) -> p c i", i=RUN),
-                MULT,
-            )
-        for a, b in ((FUSED, FUSED + late_width), (FUSED + late_width, SLOTS)):
-            nc.gpsimd.tensor_scalar(woven(a, b), part(fused, FUSED, a, b).rearrange("p t c i -> p c t i"), 1.0, 0.0, MULT, ADD)
+        nc.vector.tensor_copy(gathered(MIDDLE - HEAD, MIDDLE)[:, 0], looked_up(0, MIDDLE - HEAD, MIDDLE))
+        for t in range(R):
+            for a, b in pieces(FUSED, half, SLOTS) if t == 0 else pieces(FUSED, SLOTS):
+                nc.vector.tensor_tensor(
+                    gathered(a, b)[:, t],
+                    looked_up(t, a, b),
+                    gate_fused[:, a - FUSED : b - FUSED].rearrange("p (c i) -> p c i", i=RUN),
+                    MULT,
+                )
+        for a, b in pieces(FUSED, FUSED + late_width, SLOTS):
+            nc.gpsimd.tensor_scalar(woven(a, b), by_runs(a, b), 1.0, 0.0, MULT, ADD)
 
-        for t in ARRIVAL[1:]:
-            scalar_gather(middle, EARLY, t, EARLY, LATE)
-        for t in ARRIVAL:
-            scalar_gather(late, LATE, t, LATE, FUSED)
-        dx = keep.tile([P, SLOTS], F32, name="dx", tag=f"plane{ARRIVAL[3]}", align_bytes=256)
+        for t in range(1, R):
+            scalar_gather(t, MIDDLE, LATE)
+        for t in range(R):
+            scalar_gather(t, LATE, FUSED)
+        dx = keep.tile([P, SLOTS], F32, name="dx", tag=f"plane{R - 1}", align_bytes=256)
 
-        for a, b in ((0, 512), (512, 1024), (1024, 1536), (1536, EARLY)):
-            weigh(early, 0, a, b)
-        weigh(middle, EARLY, EARLY, LATE)
-        quantise(0, 1024)
-        multiply(0, 512, banks[0])
-        multiply(512, 1024, banks[1])
-        quantise(1024, 2048)
-        multiply(1024, 1536, banks[2])
-        multiply(1536, 2048, banks[3])
-        quantise(FUSED, 3072)
-        quantise(3072, SLOTS)
-        multiply(FUSED, 3072, banks[6])
+        for a in range(0, LATE, C):
+            vector_weigh(a, a + C)
+        for a in range(0, LATE, 2 * C):
+            quantise(a, a + 2 * C)
+            for e in (a // C, a // C + 1):
+                multiply(e * C, (e + 1) * C, banks[e])
+        quantise(FUSED, 6 * C)
+        quantise(6 * C, SLOTS)
+        multiply(FUSED, 6 * C, banks[6])
         for e in range(4):
-            empty(e * C, (e + 1) * C, banks[e])
-        empty(FUSED, 3072, banks[6])
+            empty(nc.scalar.copy, e * C, (e + 1) * C, banks[e])
+        empty(nc.scalar.copy, FUSED, 6 * C, banks[6])
         for e in (6, 7):
             multiply(e * C, (e + 1) * C, banks[e - 6])
-            empty(e * C, (e + 1) * C, banks[e - 6])
-        weigh(late, LATE, *SHARE)
-        weigh(late, LATE, 2048, 2304)
-        weigh(late, LATE, 2560, 2816)
-        for a, b, bank in ((2048, 2304, 4), (2560, 2816, 5), (2304, 2560, 2)):
+            empty(nc.scalar.copy, e * C, (e + 1) * C, banks[e - 6])
+
+        weigh(nc.gpsimd, SHARE[0], SHARE[1], gate_share[:])
+        vector_weigh(LATE, SHARE[0])
+        vector_weigh(SHARE[1], FUSED)
+        last = tuple(zip(pieces(LATE, LATE + 256, LATE + C, FUSED - P, FUSED), (banks[4], banks[2], banks[5], banks[7])))
+        for (a, b), bank in last:
             quantise(a, b)
-            multiply(a, b, banks[bank])
-        empty(2048, 2304, banks[4])
-        empty(2560, 2816, banks[5])
-        empty(2304, 2560, banks[2], nc.vector.tensor_copy)
+            multiply(a, b, bank)
+        for (a, b), bank in last:
+            empty(nc.vector.tensor_copy if a == LATE else nc.scalar.copy, a, b, bank)
 
         def results(pos_sb, a, b):
             return dx[:].indirect(pos_sb[:, a // 16 : b // 16])
 
-        first, both = 320, 1792
-        nc.vector.tensor_copy(res1[:, :first], results(pos1_sb, 0, first))
-        for a, b in ((first, 576), (576, 1088), (1088, 1600), (1600, T)):
-            nc.scalar.activation(res1[:, a:b], results(pos1_sb, a, b), COPY)
-        nc.scalar.activation(total[:, both:], results(pos2_sb, both, T), COPY)
-        nc.vector.tensor_tensor(total[:, first:576], results(pos2_sb, first, 576), res1[:, first:576], ADD)
-        for a, b, end in ((0, first, 576), (576, 1088, 1088), (1088, 1600, 1600), (1600, both, both)):
+        def add_second(a, b):
             nc.vector.tensor_tensor(total[:, a:b], results(pos2_sb, a, b), res1[:, a:b], ADD)
-            nc.sync.dma_start(out[:, a:end], total[:, a:end])
-        nc.vector.tensor_tensor(total[:, both:], total[:, both:], res1[:, both:], ADD)
-        nc.sync.dma_start(out[:, both:], total[:, both:])
+
+        def store(a, b):
+            nc.sync.dma_start(out[:, a:b], total[:, a:b])
+
+        nc.vector.tensor_copy(res1[:, :FIRST], results(pos1_sb, 0, FIRST))
+        for a, b in pieces(*AHEAD):
+            nc.scalar.activation(res1[:, a:b], results(pos1_sb, a, b), COPY)
+        nc.scalar.activation(total[:, BOTH:], results(pos2_sb, BOTH, T), COPY)
+        add_second(FIRST, AHEAD[1])
+        add_second(0, FIRST)
+        store(0, AHEAD[1])
+        for a, b in pieces(*AHEAD[1:-1], BOTH):
+            add_second(a, b)
+            store(a, b)
+        nc.vector.tensor_tensor(total[:, BOTH:], total[:, BOTH:], res1[:, BOTH:], ADD)
+        store(BOTH, T)

@@ -24,11 +24,13 @@ MULT = mybir.AluOpType.mult
 ADD = mybir.AluOpType.add
 COPY = mybir.ActivationFunctionType.Copy
 
-MIDDLE = 3 * C
-LATE = 4 * C
-FUSED = 5 * C + C // 2
-HEAD = 416
-SHARE = (LATE + 320, LATE + C)
+A1 = (0, 640)
+A2 = (640, 1536)
+OWN = (1536, 3328)
+KEPT = 2944
+LATE = (3328, SLOTS)
+SHARE = (3776, 3968)
+OPENING = 1024
 FIRST = 320
 BOTH = 1792
 AHEAD = (FIRST, FIRST + 256, FIRST + 256 + C, FIRST + 256 + 2 * C, T)
@@ -36,6 +38,10 @@ AHEAD = (FIRST, FIRST + 256, FIRST + 256 + C, FIRST + 256 + 2 * C, T)
 
 def pieces(*cuts):
     return tuple(zip(cuts, cuts[1:]))
+
+
+def width(span):
+    return span[1] - span[0]
 
 
 def tile_moe_bdx_lin_none_kernel(tc, dyT, w_words, w_scales, gate, offs, pos1, pos2, out):
@@ -54,22 +60,30 @@ def tile_moe_bdx_lin_none_kernel(tc, dyT, w_words, w_scales, gate, offs, pos1, p
         scales = keep.tile([P, SLOTS], U8, name="scales", align_bytes=64)
         res1 = keep.tile([P, T], F32, name="res1")
         total = keep.tile([P, T], F32, name="total")
-        grouped = keep.tile([P, SLOTS, R], BF16, name="grouped", align_bytes=256)
+        paired = keep.tile([P, A2[1], R], BF16, name="paired", align_bytes=256)
+        grouped = keep.tile([P, LATE[0] - OWN[0], R], BF16, name="grouped", align_bytes=256)
 
-        middle_width, late_width, fused_width = LATE - MIDDLE, FUSED - LATE, SLOTS - FUSED
-        early = keep.tile([P, R, MIDDLE // RUN, RUN], F32, name="early")
-        fused = keep.tile([P, R, fused_width // RUN, RUN], F32, name="fused")
-        late = fused[:, :, : late_width // RUN, :]
-        middle_flat = keep.tile([P, R * middle_width], F32, name="middle_flat", align_bytes=256)
-        middle = middle_flat[:].rearrange("p (t c i) -> p t c i", t=R, i=RUN)
-        gate_fused = middle_flat[:, middle_width : middle_width + fused_width]
-        gate_share = keep.tile([P, SHARE[1] - SHARE[0]], F32, name="gate_share")
+        low = keep.tile([P, 2, A2[1] // RUN, RUN], F32, name="low", align_bytes=256)
+        late = keep.tile([P, R, width(LATE) // RUN, RUN], F32, name="late", align_bytes=256)
+        high2 = keep.tile([P, 2, width(A2) // RUN, RUN], F32, name="high2", align_bytes=256)
+        own = keep.tile([P, R, width(OWN) // RUN, RUN], F32, name="own", align_bytes=256)
+        gate2 = keep.tile([P, width(A2) // RUN, RUN], F32, name="gate2", align_bytes=256)
+        gates = {A1: late[:, 2, : width(A1) // RUN, :], A2: gate2[:]}
+        gate_share = keep.tile([P, width(SHARE)], F32, name="gate_share")
         zero = keep.tile([P, 1], F32, name="zero")
-        blocks = FUSED // P
-        gate_rows = keep.tile([P, P], F32, name="gate_rows")
-        gate_col = keep.tile([P, blocks], F32, name="gate_col")
+        gate_rows = low[:, 0, OPENING // RUN : (OPENING + P) // RUN, :].rearrange("p c i -> p (c i)")
+        gate_col = keep.tile([P, SLOTS // P], F32, name="gate_col")
         ident = keep.tile([P, P], F32, name="ident")
         banks = [psum.tile([P, C], F32, name=f"bank{b}") for b in range(E)]
+
+        staged = {
+            (A1, 0): low[:, :, : A1[1] // RUN, :],
+            (A2, 0): low[:, :, A2[0] // RUN :, :],
+            (A1, 2): late[:, :2, : width(A1) // RUN, :],
+            (A2, 2): high2[:],
+            (OWN, 0): own[:],
+            (LATE, 0): late[:],
+        }
 
         nc.vector.memset(zero[:], 0.0)
         nc.vector.memset(gate_rows[32:64, :], 0.0)
@@ -78,14 +92,14 @@ def tile_moe_bdx_lin_none_kernel(tc, dyT, w_words, w_scales, gate, offs, pos1, p
         nc.vector.memset(ws_sb[:].bitcast(I32), 0)
 
         rows = dyT.rearrange("(p t) w -> p t w", t=R)
-        half = FUSED + fused_width // 2
-        nc.scalar.dma_start(gate_rows[: SLOTS // P, :], gate[0, :].rearrange("(b p) -> b p", p=P))
         nc.sync.dma_start(planes[0][:], rows[:, 0, :])
         nc.sync.dma_start(offs_sb[:], offs)
-        for a, b in pieces(FUSED, half, SLOTS):
-            nc.sync.dma_start(gate_fused[:, a - FUSED : b - FUSED], gate[0:P, a:b])
-        for t in range(1, R):
-            nc.sync.dma_start(planes[t][:], rows[:, t, :])
+        nc.sync.dma_start(planes[1][:], rows[:, 1, :])
+        nc.sync.dma_start(gate_rows[: SLOTS // P, :], gate[0, :].rearrange("(b p) -> b p", p=P))
+        nc.sync.dma_start(gates[A1], gate[0:P, : A1[1]].rearrange("p (c i) -> p c i", i=RUN))
+        nc.sync.dma_start(planes[2][:], rows[:, 2, :])
+        nc.sync.dma_start(gates[A2], gate[0:P, A2[0] : A2[1]].rearrange("p (c i) -> p c i", i=RUN))
+        nc.sync.dma_start(planes[3][:], rows[:, 3, :])
         nc.sync.dma_start(gate_share[:], gate[0:P, SHARE[0] : SHARE[1]])
         nc.sync.dma_start(
             w_sb[:].bitcast(I32).rearrange("p (e n) -> p e n", e=E),
@@ -99,32 +113,25 @@ def tile_moe_bdx_lin_none_kernel(tc, dyT, w_words, w_scales, gate, offs, pos1, p
         nc.sync.dma_start(pos1_sb[:], pos1)
         nc.sync.dma_start(pos2_sb[:], pos2)
 
-        def gathered(a, b):
-            region, first = [(r, f) for r, f in ((early, 0), (middle, MIDDLE), (late, LATE), (fused, FUSED)) if f <= a][-1]
-            return region[:, :, (a - first) // RUN : (b - first) // RUN, :]
-
         def looked_up(t, a, b):
             return planes[t][:].indirect(offs_sb[:, a // 16 : b // 16])
 
+        def plane_of(span, t):
+            first = t - t % 2 if span in (A1, A2) else 0
+            return staged[span, first][:, t - first]
+
+        def scalar_gather(span, t):
+            nc.scalar.activation(plane_of(span, t), looked_up(t, *span), COPY)
+
         def rounded(a, b):
-            shift = 2 * C if LATE <= a < FUSED else 0
-            return grouped[:, a + shift : b + shift, :]
+            tile, first = (paired, LATE[0]) if a >= LATE[0] else (grouped, OWN[0]) if a >= OWN[0] else (paired, 0)
+            return tile[:, a - first : b - first, :]
 
-        def woven(a, b):
-            return rounded(a, b).rearrange("p (c i) t -> p c t i", i=RUN)
-
-        def by_runs(a, b):
-            return gathered(a, b).rearrange("p t c i -> p c t i")
-
-        def scalar_gather(t, a, b):
-            nc.scalar.activation(gathered(a, b)[:, t], looked_up(t, a, b), COPY)
-
-        def weigh(engine, a, b, weights):
-            spread = weights.rearrange("p (c i) -> p c i", i=RUN).unsqueeze(2).to_broadcast([P, (b - a) // RUN, R, RUN])
-            engine.tensor_tensor(woven(a, b), by_runs(a, b), spread, MULT)
-
-        def vector_weigh(a, b):
-            weigh(nc.vector, a, b, banks[a // C][:, a % C : a % C + b - a])
+        def weigh(engine, span, first, count, a, b, weights):
+            values = staged[span, first][:, :, (a - span[0]) // RUN : (b - span[0]) // RUN, :].rearrange("p t c i -> p c t i")
+            woven = rounded(a, b).rearrange("p (c i) t -> p c t i", i=RUN)[:, :, first : first + count, :]
+            spread = weights.unsqueeze(2).to_broadcast([P, (b - a) // RUN, count, RUN])
+            engine.tensor_tensor(woven, values, spread, MULT)
 
         def quantise(a, b):
             nc.vector.quantize_mx(
@@ -148,63 +155,72 @@ def tile_moe_bdx_lin_none_kernel(tc, dyT, w_words, w_scales, gate, offs, pos1, p
         def empty(copy, a, b, bank):
             copy(dx[:, a:b], bank[:, : b - a])
 
-        nc.tensor.transpose(banks[E - 1][:, :P], gate_rows[:], ident[:])
-        nc.scalar.copy(gate_col[:], banks[E - 1][:, :blocks])
-        for b in range(blocks):
-            if not SHARE[0] <= b * P < SHARE[1]:
-                at = b * P % C
-                nc.tensor.transpose(banks[b * P // C][:, at : at + P], gate_col[:, b : b + 1].to_broadcast([P, P]), ident[:])
+        products = [(OWN, KEPT, OWN[1], 3, 0)]
+        products.extend((OWN, a, min(a + C, KEPT), (a - OWN[0]) // C, 0) for a in range(OWN[0], KEPT, C))
+        late_products = [(LATE, LATE[0], SHARE[0], 4, 0), (LATE, SHARE[1], SLOTS, 3, C - P)]
 
-        scalar_gather(0, 0, MIDDLE - HEAD)
-        scalar_gather(0, MIDDLE, LATE)
-        scalar_gather(1, 0, MIDDLE)
-        scalar_gather(2, 0, MIDDLE)
-        for a in range(0, MIDDLE, C):
-            scalar_gather(3, a, a + C)
-
-        nc.vector.tensor_copy(gathered(MIDDLE - HEAD, MIDDLE)[:, 0], looked_up(0, MIDDLE - HEAD, MIDDLE))
-        for t in range(R):
-            for a, b in pieces(FUSED, half, SLOTS) if t == 0 else pieces(FUSED, SLOTS):
-                nc.vector.tensor_tensor(
-                    gathered(a, b)[:, t],
-                    looked_up(t, a, b),
-                    gate_fused[:, a - FUSED : b - FUSED].rearrange("p (c i) -> p c i", i=RUN),
-                    MULT,
+        nc.tensor.transpose(banks[E - 1][:, :P], gate_rows, ident[:])
+        nc.scalar.copy(gate_col[:], banks[E - 1][:, : SLOTS // P])
+        for span, a, b, bank, at in products + late_products:
+            for k, block in enumerate(range(a // P, -(-b // P))):
+                nc.tensor.transpose(
+                    banks[bank][:, at + k * P : at + (k + 1) * P], gate_col[:, block : block + 1].to_broadcast([P, P]), ident[:]
                 )
-        for a, b in pieces(FUSED, FUSED + late_width, SLOTS):
-            nc.gpsimd.tensor_scalar(woven(a, b), by_runs(a, b), 1.0, 0.0, MULT, ADD)
 
-        for t in range(1, R):
-            scalar_gather(t, MIDDLE, LATE)
+        def vector_weigh(span, a, b, bank, at):
+            weigh(nc.vector, span, 0, R, a, b, banks[bank][:, at + a % P : at + a % P + b - a].rearrange("p (c i) -> p c i", i=RUN))
+
+        def gpsimd_pair(span, first):
+            weigh(nc.gpsimd, span, first, 2, span[0], span[1], gates[span])
+
+        nc.scalar.activation(low[:, 0, : OPENING // RUN, :], looked_up(0, 0, OPENING), COPY)
+        scalar_gather(A1, 1)
+        gpsimd_pair(A1, 0)
+        nc.scalar.activation(low[:, 0, OPENING // RUN :, :], looked_up(0, OPENING, A2[1]), COPY)
+        scalar_gather(A2, 1)
+        gpsimd_pair(A2, 0)
+        def own_last(a, b):
+            return plane_of(OWN, R - 1)[:, (a - OWN[0]) // RUN : (b - OWN[0]) // RUN, :], looked_up(R - 1, a, b)
+
+        for t in range(R - 1):
+            nc.vector.tensor_copy(plane_of(OWN, t), looked_up(t, *OWN))
+        nc.vector.tensor_copy(*own_last(KEPT, OWN[1]))
+        scalar_gather(A1, 2)
+        scalar_gather(A2, 2)
+        scalar_gather(A1, 3)
+        gpsimd_pair(A1, 2)
+        handed = [(a, b) for span, a, b, bank, at in products[1:]]
+        nc.scalar.activation(*own_last(*handed[0]), COPY)
+        scalar_gather(A2, 3)
+        gpsimd_pair(A2, 2)
+        for a, b in handed[1:]:
+            nc.scalar.activation(*own_last(a, b), COPY)
         for t in range(R):
-            scalar_gather(t, LATE, FUSED)
+            scalar_gather(LATE, t)
         dx = keep.tile([P, SLOTS], F32, name="dx", tag=f"plane{R - 1}", align_bytes=256)
 
-        for a in range(0, LATE, C):
-            vector_weigh(a, a + C)
-        for a in range(0, LATE, 2 * C):
-            quantise(a, a + 2 * C)
-            for e in (a // C, a // C + 1):
-                multiply(e * C, (e + 1) * C, banks[e])
-        quantise(FUSED, 6 * C)
-        quantise(6 * C, SLOTS)
-        multiply(FUSED, 6 * C, banks[6])
-        for e in range(4):
-            empty(nc.scalar.copy, e * C, (e + 1) * C, banks[e])
-        empty(nc.scalar.copy, FUSED, 6 * C, banks[6])
-        for e in (6, 7):
-            multiply(e * C, (e + 1) * C, banks[e - 6])
-            empty(nc.scalar.copy, e * C, (e + 1) * C, banks[e - 6])
-
-        weigh(nc.gpsimd, SHARE[0], SHARE[1], gate_share[:])
-        vector_weigh(LATE, SHARE[0])
-        vector_weigh(SHARE[1], FUSED)
-        last = tuple(zip(pieces(LATE, LATE + 256, LATE + C, FUSED - P, FUSED), (banks[4], banks[2], banks[5], banks[7])))
-        for (a, b), bank in last:
+        for product in products:
+            vector_weigh(*product)
+        early = ((3 * C, 4 * C, 0), (4 * C, 5 * C, 1), (5 * C, 6 * C, 2), (6 * C, LATE[0], 5), (2 * C, 3 * C, 6), (0, C, 7), (C, 2 * C, 0))
+        for a, b in ((3 * C, 5 * C), (5 * C, 6 * C), (6 * C, LATE[0]), (2 * C, 3 * C), (0, 2 * C)):
             quantise(a, b)
-            multiply(a, b, bank)
-        for (a, b), bank in last:
-            empty(nc.vector.tensor_copy if a == LATE else nc.scalar.copy, a, b, bank)
+        for a, b, bank in early[:-1]:
+            multiply(a, b, banks[bank])
+        for a, b, bank in early[:-1]:
+            empty(nc.scalar.copy, a, b, banks[bank])
+        a, b, bank = early[-1]
+        multiply(a, b, banks[bank])
+        empty(nc.scalar.copy, a, b, banks[bank])
+
+        weigh(nc.gpsimd, LATE, 0, R, SHARE[0], SHARE[1], gate_share[:].rearrange("p (c i) -> p c i", i=RUN))
+        for product in late_products:
+            vector_weigh(*product)
+        last = ((LATE[0], 7 * C, 4), (SHARE[1], SLOTS, 3), (7 * C, 7 * C + 256, 1), (7 * C + 256, SHARE[1], 2))
+        for a, b, bank in last:
+            quantise(a, b)
+            multiply(a, b, banks[bank])
+        for a, b, bank in last:
+            empty(nc.vector.tensor_copy if a == LATE[0] else nc.scalar.copy, a, b, banks[bank])
 
         def results(pos_sb, a, b):
             return dx[:].indirect(pos_sb[:, a // 16 : b // 16])

@@ -24,10 +24,10 @@ MULT = mybir.AluOpType.mult
 ADD = mybir.AluOpType.add
 COPY = mybir.ActivationFunctionType.Copy
 
-A1 = (0, 640)
-A2 = (640, 1536)
-OWN = (1536, 3328)
-KEPT = 2944
+A1 = (0, 896)
+A2 = (896, 1792)
+OWN = (1792, 3328)
+KEPT = 2816
 LATE = (3328, SLOTS)
 SHARE = (3776, 3968)
 OPENING = 1024
@@ -64,14 +64,14 @@ def tile_moe_bdx_lin_none_kernel(tc, dyT, w_words, w_scales, gate, offs, pos1, p
         grouped = keep.tile([P, LATE[0] - OWN[0], R], BF16, name="grouped", align_bytes=256)
 
         low = keep.tile([P, 2, A2[1] // RUN, RUN], F32, name="low", align_bytes=256)
-        late = keep.tile([P, R, width(LATE) // RUN, RUN], F32, name="late", align_bytes=256)
+        late = keep.tile([P, R, width(A1) // RUN, RUN], F32, name="late", align_bytes=256)
         high2 = keep.tile([P, 2, width(A2) // RUN, RUN], F32, name="high2", align_bytes=256)
         own = keep.tile([P, R, width(OWN) // RUN, RUN], F32, name="own", align_bytes=256)
         gate2 = keep.tile([P, width(A2) // RUN, RUN], F32, name="gate2", align_bytes=256)
         gates = {A1: late[:, 2, : width(A1) // RUN, :], A2: gate2[:]}
         gate_share = keep.tile([P, width(SHARE)], F32, name="gate_share")
         zero = keep.tile([P, 1], F32, name="zero")
-        gate_rows = low[:, 0, OPENING // RUN : (OPENING + P) // RUN, :].rearrange("p c i -> p (c i)")
+        gate_rows = keep.tile([P, P], F32, name="gate_rows")
         gate_col = keep.tile([P, SLOTS // P], F32, name="gate_col")
         ident = keep.tile([P, P], F32, name="ident")
         banks = [psum.tile([P, C], F32, name=f"bank{b}") for b in range(E)]
@@ -82,7 +82,7 @@ def tile_moe_bdx_lin_none_kernel(tc, dyT, w_words, w_scales, gate, offs, pos1, p
             (A1, 2): late[:, :2, : width(A1) // RUN, :],
             (A2, 2): high2[:],
             (OWN, 0): own[:],
-            (LATE, 0): late[:],
+            (LATE, 0): late[:, :, : width(LATE) // RUN, :],
         }
 
         nc.vector.memset(zero[:], 0.0)
@@ -155,11 +155,11 @@ def tile_moe_bdx_lin_none_kernel(tc, dyT, w_words, w_scales, gate, offs, pos1, p
         def empty(copy, a, b, bank):
             copy(dx[:, a:b], bank[:, : b - a])
 
-        products = [(OWN, KEPT, OWN[1], 3, 0)]
+        products = [(OWN, KEPT, OWN[1], 2, 0)]
         products.extend((OWN, a, min(a + C, KEPT), (a - OWN[0]) // C, 0) for a in range(OWN[0], KEPT, C))
-        late_products = [(LATE, LATE[0], SHARE[0], 4, 0), (LATE, SHARE[1], SLOTS, 3, C - P)]
+        late_products = [(LATE, LATE[0], SHARE[0], 4, 0), (LATE, SHARE[1], SLOTS, 3, 0)]
 
-        nc.tensor.transpose(banks[E - 1][:, :P], gate_rows, ident[:])
+        nc.tensor.transpose(banks[E - 1][:, :P], gate_rows[:], ident[:])
         nc.scalar.copy(gate_col[:], banks[E - 1][:, : SLOTS // P])
         for span, a, b, bank, at in products + late_products:
             for k, block in enumerate(range(a // P, -(-b // P))):
@@ -176,7 +176,7 @@ def tile_moe_bdx_lin_none_kernel(tc, dyT, w_words, w_scales, gate, offs, pos1, p
         nc.scalar.activation(low[:, 0, : OPENING // RUN, :], looked_up(0, 0, OPENING), COPY)
         scalar_gather(A1, 1)
         gpsimd_pair(A1, 0)
-        nc.scalar.activation(low[:, 0, OPENING // RUN :, :], looked_up(0, OPENING, A2[1]), COPY)
+        nc.vector.tensor_copy(low[:, 0, OPENING // RUN :, :], looked_up(0, OPENING, A2[1]))
         scalar_gather(A2, 1)
         gpsimd_pair(A2, 0)
         def own_last(a, b):
@@ -201,8 +201,8 @@ def tile_moe_bdx_lin_none_kernel(tc, dyT, w_words, w_scales, gate, offs, pos1, p
 
         for product in products:
             vector_weigh(*product)
-        early = ((3 * C, 4 * C, 0), (4 * C, 5 * C, 1), (5 * C, 6 * C, 2), (6 * C, LATE[0], 5), (2 * C, 3 * C, 6), (0, C, 7), (C, 2 * C, 0))
-        for a, b in ((3 * C, 5 * C), (5 * C, 6 * C), (6 * C, LATE[0]), (2 * C, 3 * C), (0, 2 * C)):
+        early = ((5 * C, 6 * C, 2), (6 * C, LATE[0], 5), (4 * C, 5 * C, 0), (3 * C, 4 * C, 1), (2 * C, 3 * C, 6), (0, C, 7), (C, 2 * C, 2))
+        for a, b in ((KEPT, OWN[1]), (OWN[0], KEPT), (3 * C, OWN[0]), (2 * C, 3 * C), (0, 2 * C)):
             quantise(a, b)
         for a, b, bank in early[:-1]:
             multiply(a, b, banks[bank])
@@ -215,7 +215,7 @@ def tile_moe_bdx_lin_none_kernel(tc, dyT, w_words, w_scales, gate, offs, pos1, p
         weigh(nc.gpsimd, LATE, 0, R, SHARE[0], SHARE[1], gate_share[:].rearrange("p (c i) -> p c i", i=RUN))
         for product in late_products:
             vector_weigh(*product)
-        last = ((LATE[0], 7 * C, 4), (SHARE[1], SLOTS, 3), (7 * C, 7 * C + 256, 1), (7 * C + 256, SHARE[1], 2))
+        last = ((LATE[0], 7 * C, 4), (SHARE[1], SLOTS, 3), (7 * C, 7 * C + 256, 1), (7 * C + 256, SHARE[1], 0))
         for a, b, bank in last:
             quantise(a, b)
             multiply(a, b, banks[bank])

@@ -24,12 +24,12 @@ MULT = mybir.AluOpType.mult
 ADD = mybir.AluOpType.add
 COPY = mybir.ActivationFunctionType.Copy
 
-A1 = (0, 896)
-A2 = (896, 1792)
+A1 = (0, 640)
+A2 = (640, 1792)
 OWN = (1792, 3328)
-KEPT = 2816
+KEPT = 2688
 LATE = (3328, SLOTS)
-SHARE = (3776, 3968)
+SHARE = (3840, SLOTS)
 OPENING = 1024
 FIRST = 320
 BOTH = 1792
@@ -64,7 +64,7 @@ def tile_moe_bdx_lin_none_kernel(tc, dyT, w_words, w_scales, gate, offs, pos1, p
         grouped = keep.tile([P, LATE[0] - OWN[0], R], BF16, name="grouped", align_bytes=256)
 
         low = keep.tile([P, 2, A2[1] // RUN, RUN], F32, name="low", align_bytes=256)
-        late = keep.tile([P, R, width(A1) // RUN, RUN], F32, name="late", align_bytes=256)
+        late = keep.tile([P, R, width(LATE) // RUN, RUN], F32, name="late", align_bytes=256)
         high2 = keep.tile([P, 2, width(A2) // RUN, RUN], F32, name="high2", align_bytes=256)
         own = keep.tile([P, R, width(OWN) // RUN, RUN], F32, name="own", align_bytes=256)
         gate2 = keep.tile([P, width(A2) // RUN, RUN], F32, name="gate2", align_bytes=256)
@@ -82,7 +82,7 @@ def tile_moe_bdx_lin_none_kernel(tc, dyT, w_words, w_scales, gate, offs, pos1, p
             (A1, 2): late[:, :2, : width(A1) // RUN, :],
             (A2, 2): high2[:],
             (OWN, 0): own[:],
-            (LATE, 0): late[:, :, : width(LATE) // RUN, :],
+            (LATE, 0): late[:],
         }
 
         nc.vector.memset(zero[:], 0.0)
@@ -155,9 +155,8 @@ def tile_moe_bdx_lin_none_kernel(tc, dyT, w_words, w_scales, gate, offs, pos1, p
         def empty(copy, a, b, bank):
             copy(dx[:, a:b], bank[:, : b - a])
 
-        products = [(OWN, KEPT, OWN[1], 2, 0)]
-        products.extend((OWN, a, min(a + C, KEPT), (a - OWN[0]) // C, 0) for a in range(OWN[0], KEPT, C))
-        late_products = [(LATE, LATE[0], SHARE[0], 4, 0), (LATE, SHARE[1], SLOTS, 3, 0)]
+        products = [(OWN, a, a + C, (a - OWN[0]) // C, 0) for a in reversed(range(OWN[0], OWN[1], C))]
+        late_products = [(LATE, LATE[0], SHARE[0], 3, 0)]
 
         nc.tensor.transpose(banks[E - 1][:, :P], gate_rows[:], ident[:])
         nc.scalar.copy(gate_col[:], banks[E - 1][:, : SLOTS // P])
@@ -189,11 +188,9 @@ def tile_moe_bdx_lin_none_kernel(tc, dyT, w_words, w_scales, gate, offs, pos1, p
         scalar_gather(A2, 2)
         scalar_gather(A1, 3)
         gpsimd_pair(A1, 2)
-        handed = [(a, b) for span, a, b, bank, at in products[1:]]
-        nc.scalar.activation(*own_last(*handed[0]), COPY)
         scalar_gather(A2, 3)
         gpsimd_pair(A2, 2)
-        for a, b in handed[1:]:
+        for a, b in ((OWN[0] + C, KEPT), (OWN[0], OWN[0] + C)):
             nc.scalar.activation(*own_last(a, b), COPY)
         for t in range(R):
             scalar_gather(LATE, t)
@@ -201,21 +198,20 @@ def tile_moe_bdx_lin_none_kernel(tc, dyT, w_words, w_scales, gate, offs, pos1, p
 
         for product in products:
             vector_weigh(*product)
-        early = ((5 * C, 6 * C, 2), (6 * C, LATE[0], 5), (4 * C, 5 * C, 0), (3 * C, 4 * C, 1), (2 * C, 3 * C, 6), (0, C, 7), (C, 2 * C, 2))
-        for a, b in ((KEPT, OWN[1]), (OWN[0], KEPT), (3 * C, OWN[0]), (2 * C, 3 * C), (0, 2 * C)):
+        early = ((6 * C, LATE[0], 2), (5 * C, 6 * C, 1), (4 * C, 5 * C, 0), (3 * C, 4 * C, 4), (2 * C, 3 * C, 5), (0, C, 6), (C, 2 * C, 7))
+        for a, b in ((OWN[1] - C, OWN[1]), (OWN[0], OWN[1] - C), (3 * C, OWN[0]), (2 * C, 3 * C), (0, 2 * C)):
             quantise(a, b)
-        for a, b, bank in early[:-1]:
+        for a, b, bank in early:
             multiply(a, b, banks[bank])
-        for a, b, bank in early[:-1]:
+        for a, b, bank in early[1:]:
             empty(nc.scalar.copy, a, b, banks[bank])
-        a, b, bank = early[-1]
-        multiply(a, b, banks[bank])
-        empty(nc.scalar.copy, a, b, banks[bank])
 
         weigh(nc.gpsimd, LATE, 0, R, SHARE[0], SHARE[1], gate_share[:].rearrange("p (c i) -> p c i", i=RUN))
         for product in late_products:
             vector_weigh(*product)
-        last = ((LATE[0], 7 * C, 4), (SHARE[1], SLOTS, 3), (7 * C, 7 * C + 256, 1), (7 * C + 256, SHARE[1], 0))
+        a, b, bank = early[0]
+        empty(nc.vector.tensor_copy, a, b, banks[bank])
+        last = ((LATE[0], 7 * C, 3), (7 * C, SHARE[0], 1), (SHARE[0], SLOTS - P, 0), (SLOTS - P, SLOTS, 4))
         for a, b, bank in last:
             quantise(a, b)
             multiply(a, b, banks[bank])

@@ -24,13 +24,15 @@ MULT = mybir.AluOpType.mult
 ADD = mybir.AluOpType.add
 COPY = mybir.ActivationFunctionType.Copy
 
-A1 = (0, 640)
-A2 = (640, 1792)
-OWN = (1792, 3328)
-KEPT = 2688
+EARLY = 1792
+LOW_CUT = 576
+HIGH_CUT = 960
+OPENING = 960
+OWN = (EARLY, 3328)
+LENT = 448
 LATE = (3328, SLOTS)
-SHARE = (3840, SLOTS)
-OPENING = 1024
+SHARE = (3328, 3584)
+LAST_CUT = 3840
 FIRST = 320
 BOTH = 1792
 AHEAD = (FIRST, FIRST + 256, FIRST + 256 + C, FIRST + 256 + 2 * C, T)
@@ -60,30 +62,18 @@ def tile_moe_bdx_lin_none_kernel(tc, dyT, w_words, w_scales, gate, offs, pos1, p
         scales = keep.tile([P, SLOTS], U8, name="scales", align_bytes=64)
         res1 = keep.tile([P, T], F32, name="res1")
         total = keep.tile([P, T], F32, name="total")
-        paired = keep.tile([P, A2[1], R], BF16, name="paired", align_bytes=256)
-        grouped = keep.tile([P, LATE[0] - OWN[0], R], BF16, name="grouped", align_bytes=256)
+        grouped = keep.tile([P, LATE[0] // RUN, RUN, R], BF16, name="grouped", align_bytes=256)
 
-        low = keep.tile([P, 2, A2[1] // RUN, RUN], F32, name="low", align_bytes=256)
-        late = keep.tile([P, R, width(LATE) // RUN, RUN], F32, name="late", align_bytes=256)
-        high2 = keep.tile([P, 2, width(A2) // RUN, RUN], F32, name="high2", align_bytes=256)
+        early = keep.tile([P, R + 2, EARLY // RUN, RUN], F32, name="early", align_bytes=256)
+        gate_early = early[:, R]
+        late = early[:, 2:, : width(LATE) // RUN, :]
         own = keep.tile([P, R, width(OWN) // RUN, RUN], F32, name="own", align_bytes=256)
-        gate2 = keep.tile([P, width(A2) // RUN, RUN], F32, name="gate2", align_bytes=256)
-        gates = {A1: late[:, 2, : width(A1) // RUN, :], A2: gate2[:]}
         gate_share = keep.tile([P, width(SHARE)], F32, name="gate_share")
         zero = keep.tile([P, 1], F32, name="zero")
         gate_rows = keep.tile([P, P], F32, name="gate_rows")
         gate_col = keep.tile([P, SLOTS // P], F32, name="gate_col")
         ident = keep.tile([P, P], F32, name="ident")
         banks = [psum.tile([P, C], F32, name=f"bank{b}") for b in range(E)]
-
-        staged = {
-            (A1, 0): low[:, :, : A1[1] // RUN, :],
-            (A2, 0): low[:, :, A2[0] // RUN :, :],
-            (A1, 2): late[:, :2, : width(A1) // RUN, :],
-            (A2, 2): high2[:],
-            (OWN, 0): own[:],
-            (LATE, 0): late[:],
-        }
 
         nc.vector.memset(zero[:], 0.0)
         nc.vector.memset(gate_rows[32:64, :], 0.0)
@@ -96,9 +86,9 @@ def tile_moe_bdx_lin_none_kernel(tc, dyT, w_words, w_scales, gate, offs, pos1, p
         nc.sync.dma_start(offs_sb[:], offs)
         nc.sync.dma_start(planes[1][:], rows[:, 1, :])
         nc.sync.dma_start(gate_rows[: SLOTS // P, :], gate[0, :].rearrange("(b p) -> b p", p=P))
-        nc.sync.dma_start(gates[A1], gate[0:P, : A1[1]].rearrange("p (c i) -> p c i", i=RUN))
+        nc.sync.dma_start(gate_early[:, : LOW_CUT // RUN, :], gate[0:P, :LOW_CUT].rearrange("p (c i) -> p c i", i=RUN))
         nc.sync.dma_start(planes[2][:], rows[:, 2, :])
-        nc.sync.dma_start(gates[A2], gate[0:P, A2[0] : A2[1]].rearrange("p (c i) -> p c i", i=RUN))
+        nc.sync.dma_start(gate_early[:, LOW_CUT // RUN :, :], gate[0:P, LOW_CUT:EARLY].rearrange("p (c i) -> p c i", i=RUN))
         nc.sync.dma_start(planes[3][:], rows[:, 3, :])
         nc.sync.dma_start(gate_share[:], gate[0:P, SHARE[0] : SHARE[1]])
         nc.sync.dma_start(
@@ -116,20 +106,23 @@ def tile_moe_bdx_lin_none_kernel(tc, dyT, w_words, w_scales, gate, offs, pos1, p
         def looked_up(t, a, b):
             return planes[t][:].indirect(offs_sb[:, a // 16 : b // 16])
 
-        def plane_of(span, t):
-            first = t - t % 2 if span in (A1, A2) else 0
-            return staged[span, first][:, t - first]
+        def gathered(a, b):
+            region, first = [(r, f) for r, f in ((early, 0), (own, OWN[0]), (late, LATE[0])) if f <= a][-1]
+            return region[:, :R, (a - first) // RUN : (b - first) // RUN, :]
 
-        def scalar_gather(span, t):
-            nc.scalar.activation(plane_of(span, t), looked_up(t, *span), COPY)
+        def scalar_gather(t, a, b):
+            nc.scalar.activation(gathered(a, b)[:, t], looked_up(t, a, b), COPY)
+
+        def vector_gather(t, a, b):
+            nc.vector.tensor_copy(gathered(a, b)[:, t], looked_up(t, a, b))
 
         def rounded(a, b):
-            tile, first = (paired, LATE[0]) if a >= LATE[0] else (grouped, OWN[0]) if a >= OWN[0] else (paired, 0)
-            return tile[:, a - first : b - first, :]
+            shift = -LATE[0] if a >= LATE[0] else 0
+            return grouped[:, (a + shift) // RUN : (b + shift) // RUN]
 
-        def weigh(engine, span, first, count, a, b, weights):
-            values = staged[span, first][:, :, (a - span[0]) // RUN : (b - span[0]) // RUN, :].rearrange("p t c i -> p c t i")
-            woven = rounded(a, b).rearrange("p (c i) t -> p c t i", i=RUN)[:, :, first : first + count, :]
+        def weigh(engine, first, count, a, b, weights):
+            values = gathered(a, b)[:, first : first + count].rearrange("p t c i -> p c t i")
+            woven = rounded(a, b)[:, :, :, first : first + count].rearrange("p c i t -> p c t i")
             spread = weights.unsqueeze(2).to_broadcast([P, (b - a) // RUN, count, RUN])
             engine.tensor_tensor(woven, values, spread, MULT)
 
@@ -137,7 +130,7 @@ def tile_moe_bdx_lin_none_kernel(tc, dyT, w_words, w_scales, gate, offs, pos1, p
             nc.vector.quantize_mx(
                 out=codes[:, a:b].bitcast(E5M2X4),
                 scales=scales[:, a:b],
-                in_=rounded(a, b).rearrange("p c t -> p (c t)"),
+                in_=rounded(a, b).rearrange("p c i t -> p (c i t)"),
             )
 
         def multiply(a, b, bank):
@@ -155,68 +148,69 @@ def tile_moe_bdx_lin_none_kernel(tc, dyT, w_words, w_scales, gate, offs, pos1, p
         def empty(copy, a, b, bank):
             copy(dx[:, a:b], bank[:, : b - a])
 
-        products = [(OWN, a, a + C, (a - OWN[0]) // C, 0) for a in reversed(range(OWN[0], OWN[1], C))]
-        late_products = [(LATE, LATE[0], SHARE[0], 3, 0)]
+        products = [(a, a + C, (a - OWN[0]) // C) for a in reversed(range(OWN[0], OWN[1], C))]
+        late_products = [(SHARE[1], LAST_CUT, 3), (LAST_CUT, SLOTS, 4)]
 
         nc.tensor.transpose(banks[E - 1][:, :P], gate_rows[:], ident[:])
         nc.scalar.copy(gate_col[:], banks[E - 1][:, : SLOTS // P])
-        for span, a, b, bank, at in products + late_products:
+        for a, b, bank in products + late_products:
             for k, block in enumerate(range(a // P, -(-b // P))):
                 nc.tensor.transpose(
-                    banks[bank][:, at + k * P : at + (k + 1) * P], gate_col[:, block : block + 1].to_broadcast([P, P]), ident[:]
+                    banks[bank][:, k * P : (k + 1) * P], gate_col[:, block : block + 1].to_broadcast([P, P]), ident[:]
                 )
 
-        def vector_weigh(span, a, b, bank, at):
-            weigh(nc.vector, span, 0, R, a, b, banks[bank][:, at + a % P : at + a % P + b - a].rearrange("p (c i) -> p c i", i=RUN))
+        def vector_weigh(a, b, bank):
+            weigh(nc.vector, 0, R, a, b, banks[bank][:, a % P : a % P + b - a].rearrange("p (c i) -> p c i", i=RUN))
 
-        def gpsimd_pair(span, first):
-            weigh(nc.gpsimd, span, first, 2, span[0], span[1], gates[span])
+        def gpsimd_pair(first, a, b):
+            weigh(nc.gpsimd, first, 2, a, b, gate_early[:, a // RUN : b // RUN, :])
 
-        nc.scalar.activation(low[:, 0, : OPENING // RUN, :], looked_up(0, 0, OPENING), COPY)
-        scalar_gather(A1, 1)
-        gpsimd_pair(A1, 0)
-        nc.vector.tensor_copy(low[:, 0, OPENING // RUN :, :], looked_up(0, OPENING, A2[1]))
-        scalar_gather(A2, 1)
-        gpsimd_pair(A2, 0)
-        def own_last(a, b):
-            return plane_of(OWN, R - 1)[:, (a - OWN[0]) // RUN : (b - OWN[0]) // RUN, :], looked_up(R - 1, a, b)
-
+        scalar_gather(0, 0, OPENING)
+        vector_gather(0, OPENING, EARLY)
+        for a, b in pieces(0, LOW_CUT, EARLY):
+            scalar_gather(1, a, b)
+            gpsimd_pair(0, a, b)
+        scalar_gather(1, OWN[0], OWN[0] + LENT)
+        vector_gather(0, *OWN)
+        vector_gather(1, OWN[0] + LENT, OWN[1])
+        vector_gather(2, *OWN)
+        vector_gather(2, HIGH_CUT, EARLY)
+        scalar_gather(2, 0, HIGH_CUT)
+        scalar_gather(3, 0, HIGH_CUT)
+        gpsimd_pair(2, 0, HIGH_CUT)
+        for a, b, bank in products[:-1]:
+            scalar_gather(3, a, b)
+        scalar_gather(3, HIGH_CUT, EARLY)
+        gpsimd_pair(2, HIGH_CUT, EARLY)
+        scalar_gather(3, *products[-1][:2])
         for t in range(R - 1):
-            nc.vector.tensor_copy(plane_of(OWN, t), looked_up(t, *OWN))
-        nc.vector.tensor_copy(*own_last(KEPT, OWN[1]))
-        scalar_gather(A1, 2)
-        scalar_gather(A2, 2)
-        scalar_gather(A1, 3)
-        gpsimd_pair(A1, 2)
-        scalar_gather(A2, 3)
-        gpsimd_pair(A2, 2)
-        for a, b in ((OWN[0] + C, KEPT), (OWN[0], OWN[0] + C)):
-            nc.scalar.activation(*own_last(a, b), COPY)
-        for t in range(R):
-            scalar_gather(LATE, t)
+            scalar_gather(t, *LATE)
+        for a, b in pieces(LATE[0], LAST_CUT, SLOTS):
+            scalar_gather(R - 1, a, b)
         dx = keep.tile([P, SLOTS], F32, name="dx", tag=f"plane{R - 1}", align_bytes=256)
 
         for product in products:
             vector_weigh(*product)
-        early = ((6 * C, LATE[0], 2), (5 * C, 6 * C, 1), (4 * C, 5 * C, 0), (3 * C, 4 * C, 4), (2 * C, 3 * C, 5), (0, C, 6), (C, 2 * C, 7))
-        for a, b in ((OWN[1] - C, OWN[1]), (OWN[0], OWN[1] - C), (3 * C, OWN[0]), (2 * C, 3 * C), (0, 2 * C)):
+        sums = ((6 * C, LATE[0], 2), (5 * C, 6 * C, 1), (4 * C, 5 * C, 0), (0, C, 6), (C, 2 * C, 7), (2 * C, 3 * C, 5), (3 * C, 4 * C, 2))
+        for a, b in ((6 * C, LATE[0]), (4 * C, 6 * C), (0, 2 * C), (2 * C, 4 * C)):
             quantise(a, b)
-        for a, b, bank in early:
+        for a, b, bank in sums[:-1]:
             multiply(a, b, banks[bank])
-        for a, b, bank in early[1:]:
+        for a, b, bank in sums[:-1]:
             empty(nc.scalar.copy, a, b, banks[bank])
+        a, b, bank = sums[-1]
+        multiply(a, b, banks[bank])
+        empty(nc.scalar.copy, a, b, banks[bank])
 
-        weigh(nc.gpsimd, LATE, 0, R, SHARE[0], SHARE[1], gate_share[:].rearrange("p (c i) -> p c i", i=RUN))
+        weigh(nc.gpsimd, 0, R, SHARE[0], SHARE[1], gate_share[:].rearrange("p (c i) -> p c i", i=RUN))
         for product in late_products:
             vector_weigh(*product)
-        a, b, bank = early[0]
-        empty(nc.vector.tensor_copy, a, b, banks[bank])
-        last = ((LATE[0], 7 * C, 3), (7 * C, SHARE[0], 1), (SHARE[0], SLOTS - P, 0), (SLOTS - P, SLOTS, 4))
+        last = ((7 * C, LAST_CUT, 3), (LATE[0], 7 * C, 1), (LAST_CUT, SLOTS - P, 0), (SLOTS - P, SLOTS, 4))
         for a, b, bank in last:
             quantise(a, b)
             multiply(a, b, banks[bank])
         for a, b, bank in last:
-            empty(nc.vector.tensor_copy if a == LATE[0] else nc.scalar.copy, a, b, banks[bank])
+            empty(nc.vector.tensor_copy if a < LAST_CUT else nc.scalar.copy, a, b, banks[bank])
 
         def results(pos_sb, a, b):
             return dx[:].indirect(pos_sb[:, a // 16 : b // 16])

@@ -25,11 +25,11 @@ ADD = mybir.AluOpType.add
 COPY = mybir.ActivationFunctionType.Copy
 
 EARLY = 1792
-LOW_CUT = 576
+LOW_CUT = 608
 HIGH_CUT = 960
 OPENING = 960
 OWN = (EARLY, 3328)
-LENT = 448
+LENT = 320
 LATE = (3328, SLOTS)
 SHARE = (3328, 3584)
 LAST_CUT = 3840

@@ -210,7 +210,7 @@ def tile_moe_bdx_lin_none_kernel(tc, dyT, w_words, w_scales, gate, offs, pos1, p
             quantise(a, b)
             multiply(a, b, banks[bank])
         for a, b, bank in last:
-            empty(nc.vector.tensor_copy if a < LAST_CUT else nc.scalar.copy, a, b, banks[bank])
+            empty(nc.vector.tensor_copy if b < SLOTS else nc.scalar.copy, a, b, banks[bank])
 
         def results(pos_sb, a, b):
             return dx[:].indirect(pos_sb[:, a // 16 : b // 16])

@@ -24,12 +24,12 @@ MULT = mybir.AluOpType.mult
 ADD = mybir.AluOpType.add
 COPY = mybir.ActivationFunctionType.Copy
 
-EARLY = 1792
-LOW_CUT = 608
+EARLY = 1856
+LOW_CUTS = (320, 960)
 HIGH_CUT = 960
 OPENING = 960
 OWN = (EARLY, 3328)
-LENT = 320
+LENT = 192
 LATE = (3328, SLOTS)
 SHARE = (3328, 3584)
 LAST_CUT = 3840
@@ -86,9 +86,10 @@ def tile_moe_bdx_lin_none_kernel(tc, dyT, w_words, w_scales, gate, offs, pos1, p
         nc.sync.dma_start(offs_sb[:], offs)
         nc.sync.dma_start(planes[1][:], rows[:, 1, :])
         nc.sync.dma_start(gate_rows[: SLOTS // P, :], gate[0, :].rearrange("(b p) -> b p", p=P))
-        nc.sync.dma_start(gate_early[:, : LOW_CUT // RUN, :], gate[0:P, :LOW_CUT].rearrange("p (c i) -> p c i", i=RUN))
+        nc.sync.dma_start(gate_early[:, : LOW_CUTS[0] // RUN, :], gate[0:P, : LOW_CUTS[0]].rearrange("p (c i) -> p c i", i=RUN))
+        nc.sync.dma_start(gate_early[:, LOW_CUTS[0] // RUN : LOW_CUTS[1] // RUN, :], gate[0:P, LOW_CUTS[0] : LOW_CUTS[1]].rearrange("p (c i) -> p c i", i=RUN))
         nc.sync.dma_start(planes[2][:], rows[:, 2, :])
-        nc.sync.dma_start(gate_early[:, LOW_CUT // RUN :, :], gate[0:P, LOW_CUT:EARLY].rearrange("p (c i) -> p c i", i=RUN))
+        nc.sync.dma_start(gate_early[:, LOW_CUTS[1] // RUN :, :], gate[0:P, LOW_CUTS[1] : EARLY].rearrange("p (c i) -> p c i", i=RUN))
         nc.sync.dma_start(planes[3][:], rows[:, 3, :])
         nc.sync.dma_start(gate_share[:], gate[0:P, SHARE[0] : SHARE[1]])
         nc.sync.dma_start(
@@ -148,7 +149,7 @@ def tile_moe_bdx_lin_none_kernel(tc, dyT, w_words, w_scales, gate, offs, pos1, p
         def empty(copy, a, b, bank):
             copy(dx[:, a:b], bank[:, : b - a])
 
-        products = [(a, a + C, (a - OWN[0]) // C) for a in reversed(range(OWN[0], OWN[1], C))]
+        products = [(max(b - C, OWN[0]), b, k) for k, b in enumerate(range(OWN[1], OWN[0], -C))]
         late_products = [(SHARE[1], LAST_CUT, 3), (LAST_CUT, SLOTS, 4)]
 
         nc.tensor.transpose(banks[E - 1][:, :P], gate_rows[:], ident[:])
@@ -167,7 +168,7 @@ def tile_moe_bdx_lin_none_kernel(tc, dyT, w_words, w_scales, gate, offs, pos1, p
 
         scalar_gather(0, 0, OPENING)
         vector_gather(0, OPENING, EARLY)
-        for a, b in pieces(0, LOW_CUT, EARLY):
+        for a, b in pieces(0, *LOW_CUTS, EARLY):
             scalar_gather(1, a, b)
             gpsimd_pair(0, a, b)
         scalar_gather(1, OWN[0], OWN[0] + LENT)
@@ -191,7 +192,7 @@ def tile_moe_bdx_lin_none_kernel(tc, dyT, w_words, w_scales, gate, offs, pos1, p
 
         for product in products:
             vector_weigh(*product)
-        sums = ((6 * C, LATE[0], 2), (5 * C, 6 * C, 1), (4 * C, 5 * C, 0), (0, C, 6), (C, 2 * C, 7), (2 * C, 3 * C, 5), (3 * C, 4 * C, 2))
+        sums = ((6 * C, LATE[0], 0), (5 * C, 6 * C, 1), (4 * C, 5 * C, 2), (0, C, 6), (C, 2 * C, 7), (2 * C, 3 * C, 5), (3 * C, 4 * C, 0))
         for a, b in ((6 * C, LATE[0]), (4 * C, 6 * C), (0, 2 * C), (2 * C, 4 * C)):
             quantise(a, b)
         for a, b, bank in sums[:-1]:
@@ -205,7 +206,7 @@ def tile_moe_bdx_lin_none_kernel(tc, dyT, w_words, w_scales, gate, offs, pos1, p
         weigh(nc.gpsimd, 0, R, SHARE[0], SHARE[1], gate_share[:].rearrange("p (c i) -> p c i", i=RUN))
         for product in late_products:
             vector_weigh(*product)
-        last = ((7 * C, LAST_CUT, 3), (LATE[0], 7 * C, 1), (LAST_CUT, SLOTS - P, 0), (SLOTS - P, SLOTS, 4))
+        last = ((7 * C, LAST_CUT, 3), (LATE[0], 7 * C, 1), (LAST_CUT, SLOTS - P, 2), (SLOTS - P, SLOTS, 4))
         for a, b, bank in last:
             quantise(a, b)
             multiply(a, b, banks[bank])

@@ -24,12 +24,11 @@ MULT = mybir.AluOpType.mult
 ADD = mybir.AluOpType.add
 COPY = mybir.ActivationFunctionType.Copy
 
-EARLY = 1856
+EARLY = 1920
 LOW_CUTS = (320, 960)
 HIGH_CUT = 960
 OPENING = 960
 OWN = (EARLY, 3328)
-LENT = 192
 LATE = (3328, SLOTS)
 SHARE = (3328, 3584)
 LAST_CUT = 3840
@@ -149,7 +148,7 @@ def tile_moe_bdx_lin_none_kernel(tc, dyT, w_words, w_scales, gate, offs, pos1, p
         def empty(copy, a, b, bank):
             copy(dx[:, a:b], bank[:, : b - a])
 
-        products = [(max(b - C, OWN[0]), b, k) for k, b in enumerate(range(OWN[1], OWN[0], -C))]
+        products = [(OWN[1] - C, OWN[1], 0), (OWN[0], OWN[1] - 2 * C, 2), (OWN[1] - 2 * C, OWN[1] - C, 1)]
         late_products = [(SHARE[1], LAST_CUT, 3), (LAST_CUT, SLOTS, 4)]
 
         nc.tensor.transpose(banks[E - 1][:, :P], gate_rows[:], ident[:])
@@ -171,19 +170,17 @@ def tile_moe_bdx_lin_none_kernel(tc, dyT, w_words, w_scales, gate, offs, pos1, p
         for a, b in pieces(0, *LOW_CUTS, EARLY):
             scalar_gather(1, a, b)
             gpsimd_pair(0, a, b)
-        scalar_gather(1, OWN[0], OWN[0] + LENT)
-        vector_gather(0, *OWN)
-        vector_gather(1, OWN[0] + LENT, OWN[1])
-        vector_gather(2, *OWN)
+        for t in range(R - 1):
+            vector_gather(t, *OWN)
         vector_gather(2, HIGH_CUT, EARLY)
         scalar_gather(2, 0, HIGH_CUT)
         scalar_gather(3, 0, HIGH_CUT)
         gpsimd_pair(2, 0, HIGH_CUT)
-        for a, b, bank in products[:-1]:
-            scalar_gather(3, a, b)
+        scalar_gather(3, *products[0][:2])
         scalar_gather(3, HIGH_CUT, EARLY)
         gpsimd_pair(2, HIGH_CUT, EARLY)
-        scalar_gather(3, *products[-1][:2])
+        for a, b, bank in products[1:]:
+            scalar_gather(3, a, b)
         for t in range(R - 1):
             scalar_gather(t, *LATE)
         for a, b in pieces(LATE[0], LAST_CUT, SLOTS):
@@ -211,7 +208,7 @@ def tile_moe_bdx_lin_none_kernel(tc, dyT, w_words, w_scales, gate, offs, pos1, p
             quantise(a, b)
             multiply(a, b, banks[bank])
         for a, b, bank in last:
-            empty(nc.vector.tensor_copy if b < SLOTS else nc.scalar.copy, a, b, banks[bank])
+            empty(nc.vector.tensor_copy if a < LAST_CUT else nc.scalar.copy, a, b, banks[bank])
 
         def results(pos_sb, a, b):
             return dx[:].indirect(pos_sb[:, a // 16 : b // 16])

@@ -61,12 +61,12 @@ def tile_moe_bdx_lin_none_kernel(tc, dyT, w_words, w_scales, gate, offs, pos1, p
         scales = keep.tile([P, SLOTS], U8, name="scales", align_bytes=64)
         res1 = keep.tile([P, T], F32, name="res1")
         total = keep.tile([P, T], F32, name="total")
-        grouped = keep.tile([P, LATE[0] // RUN, RUN, R], BF16, name="grouped", align_bytes=256)
+        grouped = keep.tile([P, LATE[0] // RUN, 2, RUN // 2, R], BF16, name="grouped", align_bytes=256)
 
-        early = keep.tile([P, R + 2, EARLY // RUN, RUN], F32, name="early", align_bytes=256)
+        early = keep.tile([P, R + 2, EARLY // RUN, 2, RUN // 2], F32, name="early", align_bytes=256)
         gate_early = early[:, R]
-        late = early[:, 2:, : width(LATE) // RUN, :]
-        own = keep.tile([P, R, width(OWN) // RUN, RUN], F32, name="own", align_bytes=256)
+        late = early[:, 2:, : width(LATE) // RUN]
+        own = keep.tile([P, R, width(OWN) // 2, 2], F32, name="own", align_bytes=256)
         gate_share = keep.tile([P, width(SHARE)], F32, name="gate_share")
         zero = keep.tile([P, 1], F32, name="zero")
         gate_rows = keep.tile([P, P], F32, name="gate_rows")
@@ -85,10 +85,10 @@ def tile_moe_bdx_lin_none_kernel(tc, dyT, w_words, w_scales, gate, offs, pos1, p
         nc.sync.dma_start(offs_sb[:], offs)
         nc.sync.dma_start(planes[1][:], rows[:, 1, :])
         nc.sync.dma_start(gate_rows[: SLOTS // P, :], gate[0, :].rearrange("(b p) -> b p", p=P))
-        nc.sync.dma_start(gate_early[:, : LOW_CUTS[0] // RUN, :], gate[0:P, : LOW_CUTS[0]].rearrange("p (c i) -> p c i", i=RUN))
-        nc.sync.dma_start(gate_early[:, LOW_CUTS[0] // RUN : LOW_CUTS[1] // RUN, :], gate[0:P, LOW_CUTS[0] : LOW_CUTS[1]].rearrange("p (c i) -> p c i", i=RUN))
+        nc.sync.dma_start(gate_early[:, : LOW_CUTS[0] // RUN], gate[0:P, : LOW_CUTS[0]].rearrange("p (c h i) -> p c h i", h=2, i=RUN // 2))
+        nc.sync.dma_start(gate_early[:, LOW_CUTS[0] // RUN : LOW_CUTS[1] // RUN], gate[0:P, LOW_CUTS[0] : LOW_CUTS[1]].rearrange("p (c h i) -> p c h i", h=2, i=RUN // 2))
         nc.sync.dma_start(planes[2][:], rows[:, 2, :])
-        nc.sync.dma_start(gate_early[:, LOW_CUTS[1] // RUN :, :], gate[0:P, LOW_CUTS[1] : EARLY].rearrange("p (c i) -> p c i", i=RUN))
+        nc.sync.dma_start(gate_early[:, LOW_CUTS[1] // RUN :], gate[0:P, LOW_CUTS[1] : EARLY].rearrange("p (c h i) -> p c h i", h=2, i=RUN // 2))
         nc.sync.dma_start(planes[3][:], rows[:, 3, :])
         nc.sync.dma_start(gate_share[:], gate[0:P, SHARE[0] : SHARE[1]])
         nc.sync.dma_start(
@@ -108,7 +108,8 @@ def tile_moe_bdx_lin_none_kernel(tc, dyT, w_words, w_scales, gate, offs, pos1, p
 
         def gathered(a, b):
             region, first = [(r, f) for r, f in ((early, 0), (own, OWN[0]), (late, LATE[0])) if f <= a][-1]
-            return region[:, :R, (a - first) // RUN : (b - first) // RUN, :]
+            step = 2 if first == OWN[0] else RUN
+            return region[:, :R, (a - first) // step : (b - first) // step]
 
         def scalar_gather(t, a, b):
             nc.scalar.activation(gathered(a, b)[:, t], looked_up(t, a, b), COPY)
@@ -120,17 +121,19 @@ def tile_moe_bdx_lin_none_kernel(tc, dyT, w_words, w_scales, gate, offs, pos1, p
             shift = -LATE[0] if a >= LATE[0] else 0
             return grouped[:, (a + shift) // RUN : (b + shift) // RUN]
 
-        def weigh(engine, first, count, a, b, weights):
-            values = gathered(a, b)[:, first : first + count].rearrange("p t c i -> p c t i")
-            woven = rounded(a, b)[:, :, :, first : first + count].rearrange("p c i t -> p c t i")
-            spread = weights.unsqueeze(2).to_broadcast([P, (b - a) // RUN, count, RUN])
+        def weigh(engine, first, count, a, b, weights, run):
+            order = "(c h) t i" if run < RUN else "c t (h i)"
+            staged = "p t c i -> p c t i" if OWN[0] <= a < OWN[1] else f"p t c h i -> p {order}"
+            values = gathered(a, b)[:, first : first + count].rearrange(staged)
+            woven = rounded(a, b)[:, :, :, :, first : first + count].rearrange(f"p c h i t -> p {order}")
+            spread = weights.unsqueeze(2).to_broadcast([P, (b - a) // run, count, run])
             engine.tensor_tensor(woven, values, spread, MULT)
 
         def quantise(a, b):
             nc.vector.quantize_mx(
                 out=codes[:, a:b].bitcast(E5M2X4),
                 scales=scales[:, a:b],
-                in_=rounded(a, b).rearrange("p c i t -> p (c i t)"),
+                in_=rounded(a, b).rearrange("p c h i t -> p (c h i t)"),
             )
 
         def multiply(a, b, bank):
@@ -160,10 +163,10 @@ def tile_moe_bdx_lin_none_kernel(tc, dyT, w_words, w_scales, gate, offs, pos1, p
                 )
 
         def vector_weigh(a, b, bank):
-            weigh(nc.vector, 0, R, a, b, banks[bank][:, a % P : a % P + b - a].rearrange("p (c i) -> p c i", i=RUN))
+            weigh(nc.vector, 0, R, a, b, banks[bank][:, a % P : a % P + b - a].rearrange("p (c i) -> p c i", i=RUN // 2), RUN // 2)
 
         def gpsimd_pair(first, a, b):
-            weigh(nc.gpsimd, first, 2, a, b, gate_early[:, a // RUN : b // RUN, :])
+            weigh(nc.gpsimd, first, 2, a, b, gate_early[:, a // RUN : b // RUN].rearrange("p c h i -> p c (h i)"), RUN)
 
         scalar_gather(0, 0, OPENING)
         vector_gather(0, OPENING, EARLY)
@@ -200,7 +203,7 @@ def tile_moe_bdx_lin_none_kernel(tc, dyT, w_words, w_scales, gate, offs, pos1, p
         multiply(a, b, banks[bank])
         empty(nc.scalar.copy, a, b, banks[bank])
 
-        weigh(nc.gpsimd, 0, R, SHARE[0], SHARE[1], gate_share[:].rearrange("p (c i) -> p c i", i=RUN))
+        weigh(nc.gpsimd, 0, R, SHARE[0], SHARE[1], gate_share[:].rearrange("p (c i) -> p c i", i=RUN), RUN)
         for product in late_products:
             vector_weigh(*product)
         last = ((7 * C, LAST_CUT, 3), (LATE[0], 7 * C, 1), (LAST_CUT, SLOTS - P, 2), (SLOTS - P, SLOTS, 4))

from contextlib import ExitStack

import concourse.mybir as mybir
from concourse.masks import make_identity

FLOPS = 2 * 512 * 128 * 4096
BYTES = 4 * 512 * 2048 + 8 * 128 * 256 + 8 * 16 * 128 + 4 * 4096 + 128 * 512 * 2 + 4 * 128 * 2048

P = 128
T, E, C, K = 2048, 8, 512, 128
SLOTS = E * C
R = 4
RUN = 4

F32 = mybir.dt.float32
BF16 = mybir.dt.bfloat16
I32 = mybir.dt.int32
U32 = mybir.dt.uint32
U16 = mybir.dt.uint16
U8 = mybir.dt.uint8
E5M2X4 = mybir.dt.float8_e5m2_x4
E2M1X4 = mybir.dt.float4_e2m1fn_x4
MULT = mybir.AluOpType.mult
ADD = mybir.AluOpType.add
COPY = mybir.ActivationFunctionType.Copy

EARLY = 1920
LOW_CUTS = (320, 960)
HIGH_CUT = 960
OPENING = 960
OWN = (EARLY, 3328)
LATE = (3328, SLOTS)
SHARE = (3328, 3584)
LAST_CUT = 3840
FIRST = 320
BOTH = 1792
AHEAD = (FIRST, FIRST + 256, FIRST + 256 + C, FIRST + 256 + 2 * C, T)


def pieces(*cuts):
    return tuple(zip(cuts, cuts[1:]))


def width(span):
    return span[1] - span[0]


def tile_moe_bdx_lin_none_kernel(tc, dyT, w_words, w_scales, gate, offs, pos1, pos2, out):
    nc = tc.nc
    with ExitStack() as ctx:
        keep = ctx.enter_context(tc.tile_pool(name="keep", bufs=1))
        psum = ctx.enter_context(tc.psum_pool(name="psum", bufs=1))

        offs_sb = keep.tile([P, SLOTS // 16], U16, name="offs_sb")
        pos1_sb = keep.tile([P, T // 16], U16, name="pos1_sb")
        pos2_sb = keep.tile([P, T // 16], U16, name="pos2_sb")
        planes = [keep.tile([P, T], F32, name=f"plane{t}", tag=f"plane{t}", align_bytes=256) for t in range(R)]
        w_sb = keep.tile([P, E * 2 * K], U8, name="w_sb", align_bytes=64)
        ws_sb = keep.tile([P, E * K], U8, name="ws_sb", align_bytes=64)
        codes = keep.tile([P, SLOTS], U32, name="codes", align_bytes=64)
        scales = keep.tile([P, SLOTS], U8, name="scales", align_bytes=64)
        res1 = keep.tile([P, T], F32, name="res1")
        total = keep.tile([P, T], F32, name="total")
        grouped = keep.tile([P, LATE[0] // RUN, 2, RUN // 2, R], BF16, name="grouped", align_bytes=256)

        early = keep.tile([P, R + 2, EARLY // RUN, 2, RUN // 2], F32, name="early", align_bytes=256)
        gate_early = early[:, R]
        late = early[:, 2:, : width(LATE) // RUN]
        own = keep.tile([P, R, width(OWN) // 2, 2], F32, name="own", align_bytes=256)
        gate_share = keep.tile([P, width(SHARE)], F32, name="gate_share")
        zero = keep.tile([P, 1], F32, name="zero")
        gate_rows = keep.tile([P, P], F32, name="gate_rows")
        gate_col = keep.tile([P, SLOTS // P], F32, name="gate_col")
        ident = keep.tile([P, P], F32, name="ident")
        banks = [psum.tile([P, C], F32, name=f"bank{b}") for b in range(E)]

        nc.vector.memset(zero[:], 0.0)
        nc.vector.memset(gate_rows[32:64, :], 0.0)
        nc.scalar.copy(gate_rows[64:, :], zero[64:, :].to_broadcast([64, P]))
        make_identity(nc, ident[:])
        nc.vector.memset(ws_sb[:].bitcast(I32), 0)

        rows = dyT.rearrange("(p t) w -> p t w", t=R)
        nc.sync.dma_start(planes[0][:], rows[:, 0, :])
        nc.sync.dma_start(offs_sb[:], offs)
        nc.sync.dma_start(planes[1][:], rows[:, 1, :])
        nc.sync.dma_start(gate_rows[: SLOTS // P, :], gate[0, :].rearrange("(b p) -> b p", p=P))
        nc.sync.dma_start(gate_early[:, : LOW_CUTS[0] // RUN], gate[0:P, : LOW_CUTS[0]].rearrange("p (c h i) -> p c h i", h=2, i=RUN // 2))
        nc.sync.dma_start(gate_early[:, LOW_CUTS[0] // RUN : LOW_CUTS[1] // RUN], gate[0:P, LOW_CUTS[0] : LOW_CUTS[1]].rearrange("p (c h i) -> p c h i", h=2, i=RUN // 2))
        nc.sync.dma_start(planes[2][:], rows[:, 2, :])
        nc.sync.dma_start(gate_early[:, LOW_CUTS[1] // RUN :], gate[0:P, LOW_CUTS[1] : EARLY].rearrange("p (c h i) -> p c h i", h=2, i=RUN // 2))
        nc.sync.dma_start(planes[3][:], rows[:, 3, :])
        nc.sync.dma_start(gate_share[:], gate[0:P, SHARE[0] : SHARE[1]])
        nc.sync.dma_start(
            w_sb[:].bitcast(I32).rearrange("p (e n) -> p e n", e=E),
            w_words.bitcast(I32).rearrange("e a p n -> p (e a) n"),
        )
        for q in range(4):
            nc.sync.dma_start(
                ws_sb[32 * q : 32 * q + 4, :].bitcast(I32).rearrange("f (e n) -> f e n", e=E),
                w_scales.bitcast(I32)[:, 0, 4 * q : 4 * q + 4, :].rearrange("e f n -> f e n"),
            )
        nc.sync.dma_start(pos1_sb[:], pos1)
        nc.sync.dma_start(pos2_sb[:], pos2)

        def looked_up(t, a, b):
            return planes[t][:].indirect(offs_sb[:, a // 16 : b // 16])

        def gathered(a, b):
            region, first = [(r, f) for r, f in ((early, 0), (own, OWN[0]), (late, LATE[0])) if f <= a][-1]
            step = 2 if first == OWN[0] else RUN
            return region[:, :R, (a - first) // step : (b - first) // step]

        def scalar_gather(t, a, b):
            nc.scalar.activation(gathered(a, b)[:, t], looked_up(t, a, b), COPY)

        def vector_gather(t, a, b):
            nc.vector.tensor_copy(gathered(a, b)[:, t], looked_up(t, a, b))

        def rounded(a, b):
            shift = -LATE[0] if a >= LATE[0] else 0
            return grouped[:, (a + shift) // RUN : (b + shift) // RUN]

        def weigh(engine, first, count, a, b, weights, run):
            order = "(c h) t i" if run < RUN else "c t (h i)"
            staged = "p t c i -> p c t i" if OWN[0] <= a < OWN[1] else f"p t c h i -> p {order}"
            values = gathered(a, b)[:, first : first + count].rearrange(staged)
            woven = rounded(a, b)[:, :, :, :, first : first + count].rearrange(f"p c h i t -> p {order}")
            spread = weights.unsqueeze(2).to_broadcast([P, (b - a) // run, count, run])
            engine.tensor_tensor(woven, values, spread, MULT)

        def quantise(a, b):
            nc.vector.quantize_mx(
                out=codes[:, a:b].bitcast(E5M2X4),
                scales=scales[:, a:b],
                in_=rounded(a, b).rearrange("p c h i t -> p (c h i t)"),
            )

        def multiply(a, b, bank):
            e = a // C
            nc.tensor.matmul_mx(
                out=bank[:, : b - a],
                lhsT=w_sb[:, e * 2 * K : (e + 1) * 2 * K].bitcast(E2M1X4),
                lhsT_scale=ws_sb[:, e * K : (e + 1) * K],
                rhs=codes[:, a:b].bitcast(E5M2X4),
                rhs_scale=scales[:, a:b],
                start=True,
                stop=True,
            )

        def empty(copy, a, b, bank):
            copy(dx[:, a:b], bank[:, : b - a])

        products = [(OWN[1] - C, OWN[1], 0), (OWN[0], OWN[1] - 2 * C, 2), (OWN[1] - 2 * C, OWN[1] - C, 1)]
        late_products = [(SHARE[1], LAST_CUT, 3), (LAST_CUT, SLOTS, 4)]

        nc.tensor.transpose(banks[E - 1][:, :P], gate_rows[:], ident[:])
        nc.scalar.copy(gate_col[:], banks[E - 1][:, : SLOTS // P])
        for a, b, bank in products + late_products:
            for k, block in enumerate(range(a // P, -(-b // P))):
                nc.tensor.transpose(
                    banks[bank][:, k * P : (k + 1) * P], gate_col[:, block : block + 1].to_broadcast([P, P]), ident[:]
                )

        def vector_weigh(a, b, bank):
            weigh(nc.vector, 0, R, a, b, banks[bank][:, a % P : a % P + b - a].rearrange("p (c i) -> p c i", i=RUN // 2), RUN // 2)

        def gpsimd_pair(first, a, b):
            weigh(nc.gpsimd, first, 2, a, b, gate_early[:, a // RUN : b // RUN].rearrange("p c h i -> p c (h i)"), RUN)

        scalar_gather(0, 0, OPENING)
        vector_gather(0, OPENING, EARLY)
        for a, b in pieces(0, *LOW_CUTS, EARLY):
            scalar_gather(1, a, b)
            gpsimd_pair(0, a, b)
        for t in range(R - 1):
            vector_gather(t, *OWN)
        vector_gather(2, HIGH_CUT, EARLY)
        scalar_gather(2, 0, HIGH_CUT)
        scalar_gather(3, 0, HIGH_CUT)
        gpsimd_pair(2, 0, HIGH_CUT)
        scalar_gather(3, *products[0][:2])
        scalar_gather(3, HIGH_CUT, EARLY)
        gpsimd_pair(2, HIGH_CUT, EARLY)
        for a, b, bank in products[1:]:
            scalar_gather(3, a, b)
        for t in range(R - 1):
            scalar_gather(t, *LATE)
        for a, b in pieces(LATE[0], LAST_CUT, SLOTS):
            scalar_gather(R - 1, a, b)
        dx = keep.tile([P, SLOTS], F32, name="dx", tag=f"plane{R - 1}", align_bytes=256)

        for product in products:
            vector_weigh(*product)
        sums = ((6 * C, LATE[0], 0), (5 * C, 6 * C, 1), (4 * C, 5 * C, 2), (0, C, 6), (C, 2 * C, 7), (2 * C, 3 * C, 5), (3 * C, 4 * C, 0))
        for a, b in ((6 * C, LATE[0]), (4 * C, 6 * C), (0, 2 * C), (2 * C, 4 * C)):
            quantise(a, b)
        for a, b, bank in sums[:-1]:
            multiply(a, b, banks[bank])
        for a, b, bank in sums[:-1]:
            empty(nc.scalar.copy, a, b, banks[bank])
        a, b, bank = sums[-1]
        multiply(a, b, banks[bank])
        empty(nc.scalar.copy, a, b, banks[bank])

        weigh(nc.gpsimd, 0, R, SHARE[0], SHARE[1], gate_share[:].rearrange("p (c i) -> p c i", i=RUN), RUN)
        for product in late_products:
            vector_weigh(*product)
        last = ((7 * C, LAST_CUT, 3), (LATE[0], 7 * C, 1), (LAST_CUT, SLOTS - P, 2), (SLOTS - P, SLOTS, 4))
        for a, b, bank in last:
            quantise(a, b)
            multiply(a, b, banks[bank])
        for a, b, bank in last:
            empty(nc.vector.tensor_copy if a < LAST_CUT else nc.scalar.copy, a, b, banks[bank])

        def results(pos_sb, a, b):
            return dx[:].indirect(pos_sb[:, a // 16 : b // 16])

        def add_second(a, b):
            nc.vector.tensor_tensor(total[:, a:b], results(pos2_sb, a, b), res1[:, a:b], ADD)

        def store(a, b):
            nc.sync.dma_start(out[:, a:b], total[:, a:b])

        nc.vector.tensor_copy(res1[:, :FIRST], results(pos1_sb, 0, FIRST))
        for a, b in pieces(*AHEAD):
            nc.scalar.activation(res1[:, a:b], results(pos1_sb, a, b), COPY)
        nc.scalar.activation(total[:, BOTH:], results(pos2_sb, BOTH, T), COPY)
        add_second(FIRST, AHEAD[1])
        add_second(0, FIRST)
        store(0, AHEAD[1])
        for a, b in pieces(*AHEAD[1:-1], BOTH):
            add_second(a, b)
            store(a, b)
        nc.vector.tensor_tensor(total[:, BOTH:], total[:, BOTH:], res1[:, BOTH:], ADD)
        store(BOTH, T)
